import numpy as np
import ml_dtypes


def mxq(x, axis, fmt="e4m3"):
    dtype, down = {"e4m3": (ml_dtypes.float8_e4m3fn, 7), "e5m2": (ml_dtypes.float8_e5m2, 14)}[fmt]
    v = np.moveaxis(np.asarray(x, np.float32).astype(ml_dtypes.bfloat16).astype(np.float64), axis, -1)
    blocks = v.reshape(v.shape[:-1] + (-1, 32))
    amax = np.abs(blocks).max(-1, keepdims=True)
    byte = np.maximum(np.where(amax > 0, np.frexp(amax)[1] - 1 + 127, 0) - down, 1)
    scale = np.exp2(byte - 127.0)
    codes = (blocks / scale).astype(np.float32).astype(dtype).astype(np.float64)
    return np.moveaxis((codes * scale).reshape(v.shape), -1, axis)


WIDE = False


def mx_kscale(k):
    if not WIDE:
        return np.ones(k)
    levels = np.array([10, -10, 5, -5, 0])
    if k % 512:
        return np.exp2(np.random.permutation(np.resize(levels, k // 32))).repeat(32)
    a = np.empty((k // 512, 16))
    for p in range(k // 512):
        a[p, :8] = np.random.permutation(np.resize(levels, 8))
        for g in range(8):
            far = levels[np.abs(levels - a[p, g]) >= 10]
            a[p, g + 8] = far[np.random.randint(len(far))]
    return np.exp2(a.ravel()).repeat(32)


def f64(x):
    return np.asarray(x).astype(np.float64)


def striped(idx):
    return np.tile(idx.reshape(-1, 16).T, (8, 1)).astype(np.uint16)


def unstriped(offs):
    return offs[:16].T.reshape(-1).astype(np.int64)


E2M1 = np.array([0.0, 0.5, 1.0, 1.5, 2.0, 3.0, 4.0, 6.0, -0.0, -0.5, -1.0, -1.5, -2.0, -3.0, -4.0, -6.0])


def pack_weight(w, fmt):
    k, n = w.shape
    w = f64(np.asarray(w, np.float32).astype(ml_dtypes.bfloat16)).reshape(k // 32, 32, n)
    amax = np.abs(w).max(1)
    if fmt == "e4m3":
        byte = np.frexp(amax)[1] - 1 + 127 - 7
    else:
        mant, ex = np.frexp(amax / 6.0)
        byte = np.where(mant > 0.5, ex, ex - 1) + 127
    byte = np.clip(np.where(amax > 0, byte, 1), 1, 254)
    scaled = (w * np.exp2(127.0 - byte)[:, None, :]).reshape(k, n).astype(np.float32)
    by_word = np.ascontiguousarray(scaled.reshape(k // 512, 128, 4, n).transpose(0, 1, 3, 2))
    if fmt == "e4m3":
        words = by_word.astype(ml_dtypes.float8_e4m3fn).view(np.uint8)
    else:
        c = by_word.astype(ml_dtypes.float4_e2m1fn).view(np.uint8) & 0xF
        words = (c[..., 0::2] | (c[..., 1::2] << 4)).reshape(k // 512, 128, 2 * n)
    return np.ascontiguousarray(words), np.ascontiguousarray(byte.astype(np.uint8).reshape(k // 512, 16, n))


def unpack_weight(words, scales, fmt):
    g, _, n = scales.shape
    words = np.ascontiguousarray(words).reshape(g, 128, n, -1)
    if fmt == "e4m3":
        vals = words.view(ml_dtypes.float8_e4m3fn).astype(np.float64)
    else:
        nib = np.empty((g, 128, n, 4), np.uint8)
        nib[..., 0::2] = words & 0xF
        nib[..., 1::2] = words >> 4
        vals = E2M1[nib]
    vals = vals * np.repeat(np.exp2(scales.astype(np.float64) - 127.0), 8, axis=1)[..., None]
    return vals.transpose(0, 1, 3, 2).reshape(g * 512, n)


def pack_table(v):
    words, scales = pack_weight(v, "e4m3")
    return np.concatenate([words.reshape(words.shape[0], -1), scales.reshape(scales.shape[0], -1)], axis=1)


def unpack_table(tab):
    g, t = tab.shape[0], tab.shape[1] // 528
    return unpack_weight(tab[:, :512 * t].reshape(g, 128, t, 4), tab[:, 512 * t:].reshape(g, 16, t), "e4m3")


K, H, M, T, S = 1536, 1024, 1024, 2048, 1024


def setup_inputs():
    n = np.random.standard_normal
    s = mx_kscale(K)[:, None]
    u = mx_kscale(H)[:, None]
    p_w2 = pack_weight(1.4 * n((H, M)) / np.sqrt(H) / u, "e2m1")
    return {
        "tab": pack_table(n((K, T)) * s),
        "w1": (n((K, H)) / np.sqrt(K) / s * u.T).astype(np.float32),
        "w2_words": p_w2[0],
        "w2_scales": p_w2[1],
        "prev": (n((1024, 1024))).astype(np.float32),
        "offs": striped(np.random.permutation(T)[:S]),
    }


def reference(tab, w1, w2_words, w2_scales, prev, offs):
    tab_ = unpack_table(tab)[:, unstriped(offs)]
    w1_ = mxq(f64(w1), 0, "e4m3")
    w2_ = unpack_weight(w2_words, w2_scales, "e2m1")
    h_ = mxq(np.maximum(w1_.T @ tab_, 0.0), 0, "e4m3")
    y = w2_.T @ h_
    return f64(prev) + y

@@ -1,0 +1,266 @@
+from contextlib import ExitStack
+
+import concourse.mybir as mybir
+
+K, H, M, T, S = 1536, 1024, 1024, 2048, 1024
+FLOPS = 2 * K * H * S + 2 * H * M * S
+
+F32 = mybir.dt.float32
+BF16 = mybir.dt.bfloat16
+I32 = mybir.dt.int32
+U32 = mybir.dt.uint32
+U16 = mybir.dt.uint16
+U8 = mybir.dt.uint8
+FP8X4 = mybir.dt.float8_e4m3fn_x4
+FP4X4 = mybir.dt.float4_e2m1fn_x4
+RELU = mybir.ActivationFunctionType.Relu
+ADD = mybir.AluOpType.add
+
+P = 128
+PASS = 512
+KA = K // PASS
+HB = H // PASS
+NS = S // 512
+NT = M // P
+PASSES = ((1,0,2), (0,1,2))
+
+
+def tile_list_tabmlp_res_kernel(tc, tab, w1, w2_words, w2_scales, prev, offs, out):
+    nc = tc.nc
+    with ExitStack() as ctx:
+        keep = ctx.enter_context(tc.tile_pool(name="keep", bufs=1))
+        ring = ctx.enter_context(tc.tile_pool(name="ring", bufs=1))
+        psum = ctx.enter_context(tc.psum_pool(name="psum", bufs=1))
+
+        offsets = keep.tile([P, S // 16], U16, name="offsets")
+        nc.sync.dma_start(offsets[:], offs)
+
+        tab_scales = keep.tile([P, T // 4], I32, name="tab_scales", align_bytes=64)
+        nc.vector.memset(tab_scales[:], 0)
+        w2_planes = keep.tile([P, HB, M // 4], I32, name="w2_planes", align_bytes=64)
+        nc.vector.memset(w2_planes[:], 0)
+        warm = keep.tile([P, 1], F32, name="warm")
+        nc.vector.memset(warm[:], 0.0)
+        nc.scalar.activation(warm[:], warm[:], RELU)
+
+        tab_bytes = tab[:, PASS * T :].rearrange("a (q t) -> a q t", t=T)
+
+        tab_words = {}
+
+        def load_tab(a):
+            tab_words[a] = keep.tile([P, T], I32, name=f"tab_words_{a}")
+            nc.sync.dma_start(
+                tab_words[a][:], tab[a, 0 : PASS * T].rearrange("(p x) -> p x", p=P).bitcast(I32)
+            )
+
+        def load_w1(a, c0, n):
+            raw = keep.tile([P, 4, n], F32, name=f"raw_{a}_{c0}")
+            nc.sync.dma_start(
+                raw[:], w1[PASS * a : PASS * (a + 1), c0 : c0 + n].rearrange("(p j) c -> p j c", j=4)
+            )
+            return raw
+
+        pieces = {}
+
+        def load_block(b, a):
+            raw = load_w1(a, PASS * b, PASS)
+            pieces[b, a] = [raw[:, :, 256 * i : 256 * (i + 1)] for i in range(2)]
+
+        def load_halves(b, a):
+            pieces[b, a] = [load_w1(a, PASS * b + 256 * i, 256)[:] for i in range(2)]
+
+        def load_rows(a):
+            raw = load_w1(a, 0, H)
+            for b in range(HB):
+                pieces[b, a] = [raw[:, :, PASS * b + 256 * i : PASS * b + 256 * (i + 1)] for i in range(2)]
+
+        load_tab(1)
+        load_tab(0)
+        for q in range(4):
+            nc.sync.dma_start(
+                tab_scales[32 * q : 32 * q + 4 * KA, :],
+                tab_bytes[:, 4 * q : 4 * q + 4, :].bitcast(I32),
+            )
+        load_block(0, 1)
+        load_block(0, 0)
+        load_block(0, 2)
+        load_tab(2)
+        load_block(1, 0)
+        load_block(1, 1)
+        load_block(1, 2)
+        w2_codes = {}
+        for b in range(HB):
+            w2_codes[b] = keep.tile([P, M // 2], I32, name=f"w2_codes_{b}", align_bytes=64)
+            nc.sync.dma_start(w2_codes[b][:], w2_words[b].bitcast(I32))
+        for q in range(4):
+            nc.sync.dma_start(
+                w2_planes[32 * q : 32 * q + 4, :, :],
+                w2_scales[:, 4 * q : 4 * q + 4, :].rearrange("b q n -> q b n").bitcast(I32),
+            )
+        prev_sb = []
+        for u in range(NT // 2):
+            prev_sb.append(keep.tile([P, 2, S], F32, name=f"prev_{u}"))
+            nc.sync.dma_start(prev_sb[u][:], prev[256 * u : 256 * (u + 1), :].rearrange("(t p) j -> p t j", p=P))
+
+        w1_codes = {}
+        w1_planes = {}
+
+        def lay_out_w1(b, a, engines):
+            grouped = ring.tile([P, 4, P, 4], BF16, name=f"grouped_{a}", align_bytes=64)
+            for i in range(2):
+                src = pieces[b, a][i].rearrange("p j (m t) -> p m j t", t=4)
+                dst = grouped[:, :, 64 * i : 64 * (i + 1), :].rearrange("p t m j -> p m j t")
+                if engines[i] == "S":
+                    nc.scalar.copy(dst, src)
+                else:
+                    nc.vector.tensor_copy(dst, src)
+            return grouped
+
+        def quantize_w1(b, a, grouped):
+            w1_codes[b, a] = keep.tile([P, PASS], U32, name=f"w1_codes_{b}_{a}", align_bytes=64)
+            w1_planes[b, a] = keep.tile([P, PASS], U8, name=f"w1_planes_{b}_{a}", align_bytes=64)
+            nc.vector.quantize_mx(
+                out=w1_codes[b, a][:].bitcast(FP8X4),
+                scales=w1_planes[b, a][:],
+                in_=grouped[:].rearrange("p t m j -> p (t m j)"),
+            )
+
+        picked = {}
+        picked_scales = keep.tile([P, S], U8, name="picked_scales", align_bytes=64)
+
+        def gather_words(a, s):
+            if a not in picked:
+                picked[a] = keep.tile([P, S], U32, name=f"picked_{a}", align_bytes=64)
+            nc.vector.tensor_copy(
+                picked[a][:, 512 * s : 512 * (s + 1)],
+                tab_words[a][:].bitcast(U32).indirect(offsets[:, 32 * s : 32 * (s + 1)]),
+            )
+
+        def gather_scales(s):
+            nc.vector.tensor_copy(
+                picked_scales[:, 512 * s : 512 * (s + 1)],
+                tab_scales[:].bitcast(U8).indirect(offsets[:, 32 * s : 32 * (s + 1)]),
+            )
+
+        def layer1(dst, b, a, j, t0, n):
+            nc.tensor.matmul_mx(
+                out=dst,
+                lhsT=w1_codes[b, a][:, P * j : P * (j + 1)].bitcast(FP8X4),
+                lhsT_scale=w1_planes[b, a][:, P * j : P * (j + 1)],
+                rhs=picked[a][:, t0 : t0 + n].bitcast(FP8X4),
+                rhs_scale=picked_scales[4 * a : P, t0 : t0 + n],
+                start=(a == PASSES[b][0]),
+                stop=(a == PASSES[b][-1]),
+            )
+
+        h_grouped = {}
+        for b in range(HB):
+            for s in range(NS):
+                h_grouped[b, s] = keep.tile([P, 512, 4], BF16, name=f"h_grouped_{b}_{s}", align_bytes=64)
+        h_codes = {}
+        h_planes = {}
+        for b in range(HB):
+            for s in range(NS):
+                h_codes[b, s] = keep.tile([P, 512], U32, name=f"h_codes_{b}_{s}", align_bytes=64)
+                h_planes[b, s] = keep.tile([P, 512], U8, name=f"h_planes_{b}_{s}", align_bytes=64)
+
+        def quantize_h(b, s, c0, n):
+            nc.vector.quantize_mx(
+                out=h_codes[b, s][:, c0 : c0 + n].bitcast(FP8X4),
+                scales=h_planes[b, s][:, c0 : c0 + n],
+                in_=h_grouped[b, s][:, c0 : c0 + n, :].rearrange("p n j -> p (n j)"),
+            )
+
+        def relu(dst, src, engine):
+            if engine == "S":
+                nc.scalar.activation(dst, src, RELU)
+            else:
+                nc.vector.tensor_scalar_max(dst, src, 0.0)
+
+        def narrow_slice(b, s, quantize, engines, first):
+            for g in range(4):
+                bank = psum.tile([P, 4, P], F32, name=f"bank{first + g}")
+                for j in range(4):
+                    for a in PASSES[b]:
+                        layer1(bank[:, j, :], b, a, j, 512 * s + P * g, P)
+                relu(h_grouped[b, s][:, P * g : P * (g + 1), :], bank[:].rearrange("p j n -> p n j"), engines[g])
+                if quantize and g % 2 == 1:
+                    quantize_h(b, s, P * (g - 1), 2 * P)
+
+        def wide_banks(first):
+            return [psum.tile([P, 512], F32, name=f"bank{first + j}") for j in range(4)]
+
+        def wide_planes(b, s, banks, engines):
+            planes = ring.tile([P, 4, 512], BF16, name=f"planes_{b}")
+            for j in range(4):
+                relu(planes[:, j, :], banks[j][:], engines[j])
+            return planes
+
+        def wide_finish(b, s, planes, engines):
+            for g in range(4):
+                cols = slice(P * g, P * (g + 1))
+                dst = h_grouped[b, s][:, cols, :].rearrange("p (c i) t -> p c t i", i=4)
+                src = planes[:, :, cols].rearrange("p t (c i) -> p c t i", i=4)
+                if engines[g] == "S":
+                    nc.scalar.copy(dst, src)
+                else:
+                    nc.vector.tensor_copy(dst, src)
+            quantize_h(b, s, 0, 512)
+
+        quantize_w1(0, 0, lay_out_w1(0, 0, "VS"))
+        gather_words(0, 1)
+        quantize_w1(0, 1, lay_out_w1(0, 1, "SS"))
+        quantize_w1(1, 1, lay_out_w1(1, 1, "SV"))
+        gather_words(2, 0)
+        gather_scales(0)
+        quantize_w1(0, 2, lay_out_w1(0, 2, "SV"))
+        gather_words(0, 0)
+        quantize_w1(1, 2, lay_out_w1(1, 2, "VS"))
+        gather_words(1, 0)
+        early0 = wide_banks(4)
+        for j in range(4):
+            layer1(early0[j][:], 0, 1, j, 0, 512)
+        for j in range(4):
+            layer1(early0[j][:], 0, 0, j, 0, 512)
+        for j in range(4):
+            layer1(early0[j][:], 0, 2, j, 0, 512)
+        gather_words(1, 1)
+        gather_words(2, 1)
+        planes0 = wide_planes(0, 0, early0, "SSSV")
+        gather_scales(1)
+        quantize_w1(1, 0, lay_out_w1(1, 0, "VV"))
+        early1 = wide_banks(4)
+        for j in range(4):
+            layer1(early1[j][:], 1, 0, j, 0, 512)
+        for j in range(4):
+            layer1(early1[j][:], 1, 1, j, 0, 512)
+        for j in range(4):
+            layer1(early1[j][:], 1, 2, j, 0, 512)
+        planes1 = wide_planes(1, 0, early1, "SSSV")
+        narrow_slice(0, 1, False, "SSSV", 0)
+        narrow_slice(1, 1, True, "VSSS", 0)
+        wide_finish(1, 0, planes1, "VVVS")
+        quantize_h(0, 1, 0, 512)
+        wide_finish(0, 0, planes0, "VSVS")
+
+        for n in range(NT):
+            result = keep.tile([P, S], F32, name=f"result_{n}")
+            for s in range(NS):
+                turn = 6 + 2 * n + s
+                cols = slice(512 * s, 512 * (s + 1))
+                bank = psum.tile([P, 512], F32, name=f"bank{turn % 8}")
+                for b in range(HB):
+                    nc.tensor.matmul_mx(
+                        out=bank[:],
+                        lhsT=w2_codes[b][:].bitcast(U8)[:, 256 * n : 256 * (n + 1)].bitcast(FP4X4),
+                        lhsT_scale=w2_planes[:, b, :].bitcast(U8)[:, P * n : P * (n + 1)],
+                        rhs=h_codes[b, s][:].bitcast(FP8X4),
+                        rhs_scale=h_planes[b, s][:],
+                        start=(b == 0),
+                        stop=(b == HB - 1),
+                    )
+                nc.vector.tensor_tensor(result[:, cols], bank[:], prev_sb[n // 2][:, n % 2, cols], ADD)
+                if n == NT - 1:
+                    nc.sync.dma_start(out[P * n : P * (n + 1), cols], result[:, cols])
+            if n < NT - 1:
+                nc.sync.dma_start(out[P * n : P * (n + 1), :], result[:])

@@ -22,14 +22,14 @@ KA = K // PASS
 HB = H // PASS
 NS = S // 512
 NT = M // P
-PASSES = ((1,0,2), (0,1,2))
+BANKS = 8
+VECTOR_SHARE = 88
 
 
 def tile_list_tabmlp_res_kernel(tc, tab, w1, w2_words, w2_scales, prev, offs, out):
     nc = tc.nc
     with ExitStack() as ctx:
         keep = ctx.enter_context(tc.tile_pool(name="keep", bufs=1))
-        ring = ctx.enter_context(tc.tile_pool(name="ring", bufs=1))
         psum = ctx.enter_context(tc.psum_pool(name="psum", bufs=1))
 
         offsets = keep.tile([P, S // 16], U16, name="offsets")
@@ -46,6 +46,7 @@ def tile_list_tabmlp_res_kernel(tc, tab, w1, w2_words, w2_scales, prev, offs, ou
         tab_bytes = tab[:, PASS * T :].rearrange("a (q t) -> a q t", t=T)
 
         tab_words = {}
+        w1_raw = {}
 
         def load_tab(a):
             tab_words[a] = keep.tile([P, T], I32, name=f"tab_words_{a}")
@@ -53,41 +54,27 @@ def tile_list_tabmlp_res_kernel(tc, tab, w1, w2_words, w2_scales, prev, offs, ou
                 tab_words[a][:], tab[a, 0 : PASS * T].rearrange("(p x) -> p x", p=P).bitcast(I32)
             )
 
-        def load_w1(a, c0, n):
-            raw = keep.tile([P, 4, n], F32, name=f"raw_{a}_{c0}")
+        def load_w1(b, a):
+            w1_raw[b, a] = keep.tile([P, 4, PASS], F32, name=f"w1_raw_{b}_{a}")
             nc.sync.dma_start(
-                raw[:], w1[PASS * a : PASS * (a + 1), c0 : c0 + n].rearrange("(p j) c -> p j c", j=4)
+                w1_raw[b, a][:],
+                w1[PASS * a : PASS * (a + 1), PASS * b : PASS * (b + 1)].rearrange("(p j) c -> p j c", j=4),
             )
-            return raw
 
-        pieces = {}
-
-        def load_block(b, a):
-            raw = load_w1(a, PASS * b, PASS)
-            pieces[b, a] = [raw[:, :, 256 * i : 256 * (i + 1)] for i in range(2)]
-
-        def load_halves(b, a):
-            pieces[b, a] = [load_w1(a, PASS * b + 256 * i, 256)[:] for i in range(2)]
-
-        def load_rows(a):
-            raw = load_w1(a, 0, H)
-            for b in range(HB):
-                pieces[b, a] = [raw[:, :, PASS * b + 256 * i : PASS * b + 256 * (i + 1)] for i in range(2)]
-
-        load_tab(1)
         load_tab(0)
+        load_tab(1)
+        load_w1(0, 0)
         for q in range(4):
             nc.sync.dma_start(
                 tab_scales[32 * q : 32 * q + 4 * KA, :],
                 tab_bytes[:, 4 * q : 4 * q + 4, :].bitcast(I32),
             )
-        load_block(0, 1)
-        load_block(0, 0)
-        load_block(0, 2)
+        load_w1(0, 1)
+        load_w1(0, 2)
         load_tab(2)
-        load_block(1, 0)
-        load_block(1, 1)
-        load_block(1, 2)
+        load_w1(1, 0)
+        load_w1(1, 1)
+        load_w1(1, 2)
         w2_codes = {}
         for b in range(HB):
             w2_codes[b] = keep.tile([P, M // 2], I32, name=f"w2_codes_{b}", align_bytes=64)
@@ -105,18 +92,14 @@ def tile_list_tabmlp_res_kernel(tc, tab, w1, w2_words, w2_scales, prev, offs, ou
         w1_codes = {}
         w1_planes = {}
 
-        def lay_out_w1(b, a, engines):
-            grouped = ring.tile([P, 4, P, 4], BF16, name=f"grouped_{a}", align_bytes=64)
-            for i in range(2):
-                src = pieces[b, a][i].rearrange("p j (m t) -> p m j t", t=4)
-                dst = grouped[:, :, 64 * i : 64 * (i + 1), :].rearrange("p t m j -> p m j t")
-                if engines[i] == "S":
-                    nc.scalar.copy(dst, src)
-                else:
-                    nc.vector.tensor_copy(dst, src)
-            return grouped
-
-        def quantize_w1(b, a, grouped):
+        def quantize_w1(b, a, on_vector):
+            grouped = keep.tile([P, 4, P, 4], BF16, name=f"grouped_{b}_{a}", align_bytes=64)
+            src = w1_raw[b, a][:].rearrange("p j (m t) -> p m j t", t=4)
+            dst = grouped[:].rearrange("p t m j -> p m j t")
+            if on_vector < P:
+                nc.scalar.copy(dst[:, on_vector:P], src[:, on_vector:P])
+            if on_vector > 0:
+                nc.vector.tensor_copy(dst[:, 0:on_vector], src[:, 0:on_vector])
             w1_codes[b, a] = keep.tile([P, PASS], U32, name=f"w1_codes_{b}_{a}", align_bytes=64)
             w1_planes[b, a] = keep.tile([P, PASS], U8, name=f"w1_planes_{b}_{a}", align_bytes=64)
             nc.vector.quantize_mx(
@@ -126,41 +109,43 @@ def tile_list_tabmlp_res_kernel(tc, tab, w1, w2_words, w2_scales, prev, offs, ou
             )
 
         picked = {}
-        picked_scales = keep.tile([P, S], U8, name="picked_scales", align_bytes=64)
+        picked_scales = {}
 
-        def gather_words(a, s):
-            if a not in picked:
-                picked[a] = keep.tile([P, S], U32, name=f"picked_{a}", align_bytes=64)
-            nc.vector.tensor_copy(
-                picked[a][:, 512 * s : 512 * (s + 1)],
-                tab_words[a][:].bitcast(U32).indirect(offsets[:, 32 * s : 32 * (s + 1)]),
-            )
+        def gather_words(a, s, n=512):
+            picked[a, s] = keep.tile([P, 512], U32, name=f"picked_{a}_{s}", align_bytes=64)
+            for c0 in range(0, 512, n):
+                first = (512 * s + c0) // 16
+                nc.vector.tensor_copy(
+                    picked[a, s][:, c0 : c0 + n],
+                    tab_words[a][:].bitcast(U32).indirect(offsets[:, first : first + n // 16]),
+                )
 
         def gather_scales(s):
+            picked_scales[s] = keep.tile([P, 512], U8, name=f"picked_scales_{s}", align_bytes=64)
             nc.vector.tensor_copy(
-                picked_scales[:, 512 * s : 512 * (s + 1)],
+                picked_scales[s][:],
                 tab_scales[:].bitcast(U8).indirect(offsets[:, 32 * s : 32 * (s + 1)]),
             )
 
-        def layer1(dst, b, a, j, t0, n):
-            nc.tensor.matmul_mx(
-                out=dst,
-                lhsT=w1_codes[b, a][:, P * j : P * (j + 1)].bitcast(FP8X4),
-                lhsT_scale=w1_planes[b, a][:, P * j : P * (j + 1)],
-                rhs=picked[a][:, t0 : t0 + n].bitcast(FP8X4),
-                rhs_scale=picked_scales[4 * a : P, t0 : t0 + n],
-                start=(a == PASSES[b][0]),
-                stop=(a == PASSES[b][-1]),
-            )
+        def layer1(bank, b, a, g):
+            cols = slice(P * (g % 4), P * (g % 4 + 1))
+            for j in range(4):
+                nc.tensor.matmul_mx(
+                    out=bank[:, j, :],
+                    lhsT=w1_codes[b, a][:, P * j : P * (j + 1)].bitcast(FP8X4),
+                    lhsT_scale=w1_planes[b, a][:, P * j : P * (j + 1)],
+                    rhs=picked[a, g // 4][:, cols].bitcast(FP8X4),
+                    rhs_scale=picked_scales[g // 4][4 * a : P, cols],
+                    start=(a == 0 and j == 0),
+                    stop=(a == KA - 1 and j == 3),
+                )
 
         h_grouped = {}
-        for b in range(HB):
-            for s in range(NS):
-                h_grouped[b, s] = keep.tile([P, 512, 4], BF16, name=f"h_grouped_{b}_{s}", align_bytes=64)
         h_codes = {}
         h_planes = {}
         for b in range(HB):
             for s in range(NS):
+                h_grouped[b, s] = keep.tile([P, 512, 4], BF16, name=f"h_grouped_{b}_{s}", align_bytes=64)
                 h_codes[b, s] = keep.tile([P, 512], U32, name=f"h_codes_{b}_{s}", align_bytes=64)
                 h_planes[b, s] = keep.tile([P, 512], U8, name=f"h_planes_{b}_{s}", align_bytes=64)
 
@@ -171,84 +156,45 @@ def tile_list_tabmlp_res_kernel(tc, tab, w1, w2_words, w2_scales, prev, offs, ou
                 in_=h_grouped[b, s][:, c0 : c0 + n, :].rearrange("p n j -> p (n j)"),
             )
 
-        def relu(dst, src, engine):
-            if engine == "S":
-                nc.scalar.activation(dst, src, RELU)
-            else:
+        def rectify(bank, b, g, on_vector):
+            dst = h_grouped[b, g // 4][:, P * (g % 4) : P * (g % 4 + 1), :]
+            src = bank[:].rearrange("p j n -> p n j")
+            if on_vector:
                 nc.vector.tensor_scalar_max(dst, src, 0.0)
+            else:
+                nc.scalar.activation(dst, src, RELU)
 
-        def narrow_slice(b, s, quantize, engines, first):
-            for g in range(4):
-                bank = psum.tile([P, 4, P], F32, name=f"bank{first + g}")
-                for j in range(4):
-                    for a in PASSES[b]:
-                        layer1(bank[:, j, :], b, a, j, 512 * s + P * g, P)
-                relu(h_grouped[b, s][:, P * g : P * (g + 1), :], bank[:].rearrange("p j n -> p n j"), engines[g])
-                if quantize and g % 2 == 1:
-                    quantize_h(b, s, P * (g - 1), 2 * P)
-
-        def wide_banks(first):
-            return [psum.tile([P, 512], F32, name=f"bank{first + j}") for j in range(4)]
-
-        def wide_planes(b, s, banks, engines):
-            planes = ring.tile([P, 4, 512], BF16, name=f"planes_{b}")
-            for j in range(4):
-                relu(planes[:, j, :], banks[j][:], engines[j])
-            return planes
-
-        def wide_finish(b, s, planes, engines):
-            for g in range(4):
-                cols = slice(P * g, P * (g + 1))
-                dst = h_grouped[b, s][:, cols, :].rearrange("p (c i) t -> p c t i", i=4)
-                src = planes[:, :, cols].rearrange("p t (c i) -> p c t i", i=4)
-                if engines[g] == "S":
-                    nc.scalar.copy(dst, src)
-                else:
-                    nc.vector.tensor_copy(dst, src)
-            quantize_h(b, s, 0, 512)
-
-        quantize_w1(0, 0, lay_out_w1(0, 0, "VS"))
-        gather_words(0, 1)
-        quantize_w1(0, 1, lay_out_w1(0, 1, "SS"))
-        quantize_w1(1, 1, lay_out_w1(1, 1, "SV"))
-        gather_words(2, 0)
-        gather_scales(0)
-        quantize_w1(0, 2, lay_out_w1(0, 2, "SV"))
         gather_words(0, 0)
-        quantize_w1(1, 2, lay_out_w1(1, 2, "VS"))
+        gather_words(0, 1)
         gather_words(1, 0)
-        early0 = wide_banks(4)
-        for j in range(4):
-            layer1(early0[j][:], 0, 1, j, 0, 512)
-        for j in range(4):
-            layer1(early0[j][:], 0, 0, j, 0, 512)
-        for j in range(4):
-            layer1(early0[j][:], 0, 2, j, 0, 512)
         gather_words(1, 1)
-        gather_words(2, 1)
-        planes0 = wide_planes(0, 0, early0, "SSSV")
+        gather_scales(0)
+        quantize_w1(0, 0, 0)
         gather_scales(1)
-        quantize_w1(1, 0, lay_out_w1(1, 0, "VV"))
-        early1 = wide_banks(4)
-        for j in range(4):
-            layer1(early1[j][:], 1, 0, j, 0, 512)
-        for j in range(4):
-            layer1(early1[j][:], 1, 1, j, 0, 512)
-        for j in range(4):
-            layer1(early1[j][:], 1, 2, j, 0, 512)
-        planes1 = wide_planes(1, 0, early1, "SSSV")
-        narrow_slice(0, 1, False, "SSSV", 0)
-        narrow_slice(1, 1, True, "VSSS", 0)
-        wide_finish(1, 0, planes1, "VVVS")
-        quantize_h(0, 1, 0, 512)
-        wide_finish(0, 0, planes0, "VSVS")
+        quantize_w1(0, 1, 0)
+        quantize_w1(0, 2, 64)
+        gather_words(2, 0, 256)
+        gather_words(2, 1, 256)
+        quantize_w1(1, 0, 128)
+        quantize_w1(1, 1, 96)
+        quantize_w1(1, 2, 64)
+
+        for b in range(HB):
+            for g in range(BANKS):
+                bank = psum.tile([P, 4, P], F32, name=f"bank{g}")
+                for a in range(KA):
+                    layer1(bank, b, a, g)
+                rectify(bank, b, g, b == HB - 1 and g % 2 == 1)
+                if b == 0 and g % 4 == 3:
+                    quantize_h(b, g // 4, 0, 512)
+                if b == 1 and g % 2 == 1:
+                    quantize_h(b, g // 4, P * (g % 4 - 1), 2 * P)
 
         for n in range(NT):
             result = keep.tile([P, S], F32, name=f"result_{n}")
             for s in range(NS):
-                turn = 6 + 2 * n + s
                 cols = slice(512 * s, 512 * (s + 1))
-                bank = psum.tile([P, 512], F32, name=f"bank{turn % 8}")
+                bank = psum.tile([P, 512], F32, name=f"bank{(NS * n + s) % BANKS}")
                 for b in range(HB):
                     nc.tensor.matmul_mx(
                         out=bank[:],

@@ -23,7 +23,6 @@ HB = H // PASS
 NS = S // 512
 NT = M // P
 BANKS = 8
-VECTOR_SHARE = 88
 
 
 def tile_list_tabmlp_res_kernel(tc, tab, w1, w2_words, w2_scales, prev, offs, out):
@@ -62,13 +61,13 @@ def tile_list_tabmlp_res_kernel(tc, tab, w1, w2_words, w2_scales, prev, offs, ou
             )
 
         load_tab(0)
-        load_tab(1)
         load_w1(0, 0)
         for q in range(4):
             nc.sync.dma_start(
                 tab_scales[32 * q : 32 * q + 4 * KA, :],
                 tab_bytes[:, 4 * q : 4 * q + 4, :].bitcast(I32),
             )
+        load_tab(1)
         load_w1(0, 1)
         load_w1(0, 2)
         load_tab(2)
@@ -100,7 +99,9 @@ def tile_list_tabmlp_res_kernel(tc, tab, w1, w2_words, w2_scales, prev, offs, ou
                 nc.scalar.copy(dst[:, on_vector:P], src[:, on_vector:P])
             if on_vector > 0:
                 nc.vector.tensor_copy(dst[:, 0:on_vector], src[:, 0:on_vector])
-            w1_codes[b, a] = keep.tile([P, PASS], U32, name=f"w1_codes_{b}_{a}", align_bytes=64)
+            w1_codes[b, a] = keep.tile(
+                [P, PASS], U32, name="tab_scales" if (b, a) == (0, 0) else f"w1_codes_{b}_{a}", align_bytes=64
+            )
             w1_planes[b, a] = keep.tile([P, PASS], U8, name=f"w1_planes_{b}_{a}", align_bytes=64)
             nc.vector.quantize_mx(
                 out=w1_codes[b, a][:].bitcast(FP8X4),
@@ -143,21 +144,15 @@ def tile_list_tabmlp_res_kernel(tc, tab, w1, w2_words, w2_scales, prev, offs, ou
         h_grouped = {}
         h_codes = {}
         h_planes = {}
-        for b in range(HB):
-            for s in range(NS):
-                h_grouped[b, s] = keep.tile([P, 512, 4], BF16, name=f"h_grouped_{b}_{s}", align_bytes=64)
-                h_codes[b, s] = keep.tile([P, 512], U32, name=f"h_codes_{b}_{s}", align_bytes=64)
-                h_planes[b, s] = keep.tile([P, 512], U8, name=f"h_planes_{b}_{s}", align_bytes=64)
-
-        def quantize_h(b, s, c0, n):
+        def quantize_h(b, c0, n):
             nc.vector.quantize_mx(
-                out=h_codes[b, s][:, c0 : c0 + n].bitcast(FP8X4),
-                scales=h_planes[b, s][:, c0 : c0 + n],
-                in_=h_grouped[b, s][:, c0 : c0 + n, :].rearrange("p n j -> p (n j)"),
+                out=h_codes[b][:, c0 : c0 + n].bitcast(FP8X4),
+                scales=h_planes[b][:, c0 : c0 + n],
+                in_=h_grouped[b][:, c0 : c0 + n, :].rearrange("p n j -> p (n j)"),
             )
 
         def rectify(bank, b, g, on_vector):
-            dst = h_grouped[b, g // 4][:, P * (g % 4) : P * (g % 4 + 1), :]
+            dst = h_grouped[b][:, P * g : P * (g + 1), :]
             src = bank[:].rearrange("p j n -> p n j")
             if on_vector:
                 nc.vector.tensor_scalar_max(dst, src, 0.0)
@@ -166,29 +161,41 @@ def tile_list_tabmlp_res_kernel(tc, tab, w1, w2_words, w2_scales, prev, offs, ou
 
         gather_words(0, 0)
         gather_words(0, 1)
+        gather_scales(0)
+        gather_scales(1)
+        quantize_w1(0, 0, 0)
         gather_words(1, 0)
         gather_words(1, 1)
-        gather_scales(0)
-        quantize_w1(0, 0, 0)
-        gather_scales(1)
-        quantize_w1(0, 1, 0)
+        quantize_w1(0, 1, 32)
         quantize_w1(0, 2, 64)
         gather_words(2, 0, 256)
         gather_words(2, 1, 256)
         quantize_w1(1, 0, 128)
-        quantize_w1(1, 1, 96)
+        quantize_w1(1, 1, 128)
         quantize_w1(1, 2, 64)
 
         for b in range(HB):
+            h_grouped[b] = keep.tile([P, S, 4], BF16, name=f"h_grouped_{b}", align_bytes=64)
+            h_codes[b] = keep.tile(
+                [P, S], U32, name=f"grouped_{HB - 1}_{KA - 1}" if b == 0 else f"h_codes_{b}", align_bytes=64
+            )
+            h_planes[b] = keep.tile([P, S], U8, name=f"h_planes_{b}", align_bytes=64)
+
+        for b in range(HB):
+            banks = [psum.tile([P, 4, P], F32, name=f"bank{g}") for g in range(BANKS)]
+            early = KA - 1 if b == 0 else 0
+            for a in range(early):
+                for g in range(BANKS):
+                    layer1(banks[g], b, a, g)
             for g in range(BANKS):
-                bank = psum.tile([P, 4, P], F32, name=f"bank{g}")
-                for a in range(KA):
+                bank = banks[g]
+                for a in range(early, KA):
                     layer1(bank, b, a, g)
                 rectify(bank, b, g, b == HB - 1 and g % 2 == 1)
-                if b == 0 and g % 4 == 3:
-                    quantize_h(b, g // 4, 0, 512)
+                if b == 0 and g == BANKS - 1:
+                    quantize_h(b, 0, S)
                 if b == 1 and g % 2 == 1:
-                    quantize_h(b, g // 4, P * (g % 4 - 1), 2 * P)
+                    quantize_h(b, P * (g - 1), 2 * P)
 
         for n in range(NT):
             result = keep.tile([P, S], F32, name=f"result_{n}")
@@ -200,8 +207,8 @@ def tile_list_tabmlp_res_kernel(tc, tab, w1, w2_words, w2_scales, prev, offs, ou
                         out=bank[:],
                         lhsT=w2_codes[b][:].bitcast(U8)[:, 256 * n : 256 * (n + 1)].bitcast(FP4X4),
                         lhsT_scale=w2_planes[:, b, :].bitcast(U8)[:, P * n : P * (n + 1)],
-                        rhs=h_codes[b, s][:].bitcast(FP8X4),
-                        rhs_scale=h_planes[b, s][:],
+                        rhs=h_codes[b][:, cols].bitcast(FP8X4),
+                        rhs_scale=h_planes[b][:, cols],
                         start=(b == 0),
                         stop=(b == HB - 1),
                     )

@@ -74,14 +74,12 @@ def tile_list_tabmlp_res_kernel(tc, tab, w1, w2_words, w2_scales, prev, offs, ou
         load_w1(1, 0)
         load_w1(1, 1)
         load_w1(1, 2)
-        w2_codes = {}
-        for b in range(HB):
-            w2_codes[b] = keep.tile([P, M // 2], I32, name=f"w2_codes_{b}", align_bytes=64)
-            nc.sync.dma_start(w2_codes[b][:], w2_words[b].bitcast(I32))
-        for q in range(4):
+        w2_codes = keep.tile([P, HB, M // 2], I32, name="w2_codes", align_bytes=64)
+        nc.sync.dma_start(w2_codes[:], w2_words.rearrange("b p x -> p b x").bitcast(I32))
+        for r in range(4):
             nc.sync.dma_start(
-                w2_planes[32 * q : 32 * q + 4, :, :],
-                w2_scales[:, 4 * q : 4 * q + 4, :].rearrange("b q n -> q b n").bitcast(I32),
+                w2_planes[r:P:32, :, :],
+                w2_scales[:, r:16:4, :].rearrange("b q n -> q b n").bitcast(I32),
             )
         prev_sb = []
         for u in range(NT // 2):
@@ -205,7 +203,7 @@ def tile_list_tabmlp_res_kernel(tc, tab, w1, w2_words, w2_scales, prev, offs, ou
                 for b in range(HB):
                     nc.tensor.matmul_mx(
                         out=bank[:],
-                        lhsT=w2_codes[b][:].bitcast(U8)[:, 256 * n : 256 * (n + 1)].bitcast(FP4X4),
+                        lhsT=w2_codes[:, b, :].bitcast(U8)[:, 256 * n : 256 * (n + 1)].bitcast(FP4X4),
                         lhsT_scale=w2_planes[:, b, :].bitcast(U8)[:, P * n : P * (n + 1)],
                         rhs=h_codes[b][:, cols].bitcast(FP8X4),
                         rhs_scale=h_planes[b][:, cols],

@@ -48,17 +48,21 @@ def tile_list_tabmlp_res_kernel(tc, tab, w1, w2_words, w2_scales, prev, offs, ou
         w1_raw = {}
 
         def load_tab(a):
-            tab_words[a] = keep.tile([P, T], I32, name=f"tab_words_{a}")
+            tab_words[a] = keep.tile([P, T], I32, name=f"tab_words_{a}", align_bytes=64)
             nc.sync.dma_start(
                 tab_words[a][:], tab[a, 0 : PASS * T].rearrange("(p x) -> p x", p=P).bitcast(I32)
             )
 
-        def load_w1(b, a):
-            w1_raw[b, a] = keep.tile([P, 4, PASS], F32, name=f"w1_raw_{b}_{a}")
+        def load_w1(first, a, count=1):
+            raw = keep.tile([P, 4, count * PASS], F32, name=f"w1_raw_{first}_{a}")
             nc.sync.dma_start(
-                w1_raw[b, a][:],
-                w1[PASS * a : PASS * (a + 1), PASS * b : PASS * (b + 1)].rearrange("(p j) c -> p j c", j=4),
+                raw[:],
+                w1[PASS * a : PASS * (a + 1), PASS * first : PASS * (first + count)].rearrange(
+                    "(p j) c -> p j c", j=4
+                ),
             )
+            for i in range(count):
+                w1_raw[first + i, a] = raw[:, :, PASS * i : PASS * (i + 1)]
 
         load_tab(0)
         load_w1(0, 0)
@@ -68,11 +72,10 @@ def tile_list_tabmlp_res_kernel(tc, tab, w1, w2_words, w2_scales, prev, offs, ou
                 tab_bytes[:, 4 * q : 4 * q + 4, :].bitcast(I32),
             )
         load_tab(1)
-        load_w1(0, 1)
+        load_w1(0, 1, HB)
         load_w1(0, 2)
         load_tab(2)
         load_w1(1, 0)
-        load_w1(1, 1)
         load_w1(1, 2)
         w2_codes = keep.tile([P, HB, M // 2], I32, name="w2_codes", align_bytes=64)
         nc.sync.dma_start(w2_codes[:], w2_words.rearrange("b p x -> p b x").bitcast(I32))
@@ -89,16 +92,18 @@ def tile_list_tabmlp_res_kernel(tc, tab, w1, w2_words, w2_scales, prev, offs, ou
         w1_codes = {}
         w1_planes = {}
 
+        reused = {(0, 0): "tab_scales", (1, 1): "tab_words_2"}
+
         def quantize_w1(b, a, on_vector):
             grouped = keep.tile([P, 4, P, 4], BF16, name=f"grouped_{b}_{a}", align_bytes=64)
-            src = w1_raw[b, a][:].rearrange("p j (m t) -> p m j t", t=4)
+            src = w1_raw[b, a].rearrange("p j (m t) -> p m j t", t=4)
             dst = grouped[:].rearrange("p t m j -> p m j t")
             if on_vector < P:
                 nc.scalar.copy(dst[:, on_vector:P], src[:, on_vector:P])
             if on_vector > 0:
                 nc.vector.tensor_copy(dst[:, 0:on_vector], src[:, 0:on_vector])
             w1_codes[b, a] = keep.tile(
-                [P, PASS], U32, name="tab_scales" if (b, a) == (0, 0) else f"w1_codes_{b}_{a}", align_bytes=64
+                [P, PASS], U32, name=reused.get((b, a), f"w1_codes_{b}_{a}"), align_bytes=64
             )
             w1_planes[b, a] = keep.tile([P, PASS], U8, name=f"w1_planes_{b}_{a}", align_bytes=64)
             nc.vector.quantize_mx(
@@ -126,6 +131,8 @@ def tile_list_tabmlp_res_kernel(tc, tab, w1, w2_words, w2_scales, prev, offs, ou
                 tab_scales[:].bitcast(U8).indirect(offsets[:, 32 * s : 32 * (s + 1)]),
             )
 
+        passes = ((0, 1, 2), (1, 0, 2))
+
         def layer1(bank, b, a, g):
             cols = slice(P * (g % 4), P * (g % 4 + 1))
             for j in range(4):
@@ -135,8 +142,8 @@ def tile_list_tabmlp_res_kernel(tc, tab, w1, w2_words, w2_scales, prev, offs, ou
                     lhsT_scale=w1_planes[b, a][:, P * j : P * (j + 1)],
                     rhs=picked[a, g // 4][:, cols].bitcast(FP8X4),
                     rhs_scale=picked_scales[g // 4][4 * a : P, cols],
-                    start=(a == 0 and j == 0),
-                    stop=(a == KA - 1 and j == 3),
+                    start=(a == passes[b][0] and j == 0),
+                    stop=(a == passes[b][-1] and j == 3),
                 )
 
         h_grouped = {}
@@ -164,13 +171,13 @@ def tile_list_tabmlp_res_kernel(tc, tab, w1, w2_words, w2_scales, prev, offs, ou
         quantize_w1(0, 0, 0)
         gather_words(1, 0)
         gather_words(1, 1)
-        quantize_w1(0, 1, 32)
-        quantize_w1(0, 2, 64)
+        quantize_w1(0, 1, 88)
+        quantize_w1(0, 2, 128)
         gather_words(2, 0, 256)
         gather_words(2, 1, 256)
+        quantize_w1(1, 1, 0)
         quantize_w1(1, 0, 128)
-        quantize_w1(1, 1, 128)
-        quantize_w1(1, 2, 64)
+        quantize_w1(1, 2, 128)
 
         for b in range(HB):
             h_grouped[b] = keep.tile([P, S, 4], BF16, name=f"h_grouped_{b}", align_bytes=64)
@@ -182,12 +189,12 @@ def tile_list_tabmlp_res_kernel(tc, tab, w1, w2_words, w2_scales, prev, offs, ou
         for b in range(HB):
             banks = [psum.tile([P, 4, P], F32, name=f"bank{g}") for g in range(BANKS)]
             early = KA - 1 if b == 0 else 0
-            for a in range(early):
+            for a in passes[b][:early]:
                 for g in range(BANKS):
                     layer1(banks[g], b, a, g)
             for g in range(BANKS):
                 bank = banks[g]
-                for a in range(early, KA):
+                for a in passes[b][early:]:
                     layer1(bank, b, a, g)
                 rectify(bank, b, g, b == HB - 1 and g % 2 == 1)
                 if b == 0 and g == BANKS - 1:
@@ -195,23 +202,24 @@ def tile_list_tabmlp_res_kernel(tc, tab, w1, w2_words, w2_scales, prev, offs, ou
                 if b == 1 and g % 2 == 1:
                     quantize_h(b, P * (g - 1), 2 * P)
 
-        for n in range(NT):
-            result = keep.tile([P, S], F32, name=f"result_{n}")
-            for s in range(NS):
-                cols = slice(512 * s, 512 * (s + 1))
-                bank = psum.tile([P, 512], F32, name=f"bank{(NS * n + s) % BANKS}")
-                for b in range(HB):
-                    nc.tensor.matmul_mx(
-                        out=bank[:],
-                        lhsT=w2_codes[:, b, :].bitcast(U8)[:, 256 * n : 256 * (n + 1)].bitcast(FP4X4),
-                        lhsT_scale=w2_planes[:, b, :].bitcast(U8)[:, P * n : P * (n + 1)],
-                        rhs=h_codes[b][:, cols].bitcast(FP8X4),
-                        rhs_scale=h_planes[b][:, cols],
-                        start=(b == 0),
-                        stop=(b == HB - 1),
-                    )
-                nc.vector.tensor_tensor(result[:, cols], bank[:], prev_sb[n // 2][:, n % 2, cols], ADD)
-                if n == NT - 1:
-                    nc.sync.dma_start(out[P * n : P * (n + 1), cols], result[:, cols])
-            if n < NT - 1:
-                nc.sync.dma_start(out[P * n : P * (n + 1), :], result[:])
+        results = [keep.tile([P, S], F32, name=f"result_{n}") for n in range(NT)]
+        turns = [(n, s) for s in range(NS) for n in range(2)]
+        turns.extend((n, s) for n in range(2, NT) for s in range(NS))
+        for turn, (n, s) in enumerate(turns):
+            cols = slice(512 * s, 512 * (s + 1))
+            bank = psum.tile([P, 512], F32, name=f"bank{turn % BANKS}")
+            for b in range(HB):
+                nc.tensor.matmul_mx(
+                    out=bank[:],
+                    lhsT=w2_codes[:, b, :].bitcast(U8)[:, 256 * n : 256 * (n + 1)].bitcast(FP4X4),
+                    lhsT_scale=w2_planes[:, b, :].bitcast(U8)[:, P * n : P * (n + 1)],
+                    rhs=h_codes[b][:, cols].bitcast(FP8X4),
+                    rhs_scale=h_planes[b][:, cols],
+                    start=(b == 0),
+                    stop=(b == HB - 1),
+                )
+            nc.vector.tensor_tensor(results[n][:, cols], bank[:], prev_sb[n // 2][:, n % 2, cols], ADD)
+            if n < 2:
+                nc.sync.dma_start(out[P * n : P * (n + 1), cols], results[n][:, cols])
+            elif s == NS - 1:
+                nc.sync.dma_start(out[P * n : P * (n + 1), :], results[n][:])

@@ -65,17 +65,16 @@ def tile_list_tabmlp_res_kernel(tc, tab, w1, w2_words, w2_scales, prev, offs, ou
                 w1_raw[first + i, a] = raw[:, :, PASS * i : PASS * (i + 1)]
 
         load_tab(0)
-        load_w1(0, 0)
+        load_tab(1)
         for q in range(4):
             nc.sync.dma_start(
                 tab_scales[32 * q : 32 * q + 4 * KA, :],
                 tab_bytes[:, 4 * q : 4 * q + 4, :].bitcast(I32),
             )
-        load_tab(1)
+        load_w1(0, 0, HB)
         load_w1(0, 1, HB)
         load_w1(0, 2)
         load_tab(2)
-        load_w1(1, 0)
         load_w1(1, 2)
         w2_codes = keep.tile([P, HB, M // 2], I32, name="w2_codes", align_bytes=64)
         nc.sync.dma_start(w2_codes[:], w2_words.rearrange("b p x -> p b x").bitcast(I32))
@@ -92,7 +91,7 @@ def tile_list_tabmlp_res_kernel(tc, tab, w1, w2_words, w2_scales, prev, offs, ou
         w1_codes = {}
         w1_planes = {}
 
-        reused = {(0, 0): "tab_scales", (1, 1): "tab_words_2"}
+        reused = {(1, 1): "tab_words_2"}
 
         def quantize_w1(b, a, on_vector):
             grouped = keep.tile([P, 4, P, 4], BF16, name=f"grouped_{b}_{a}", align_bytes=64)
@@ -131,7 +130,7 @@ def tile_list_tabmlp_res_kernel(tc, tab, w1, w2_words, w2_scales, prev, offs, ou
                 tab_scales[:].bitcast(U8).indirect(offsets[:, 32 * s : 32 * (s + 1)]),
             )
 
-        passes = ((0, 1, 2), (1, 0, 2))
+        passes = ((0, 1, 2), (0, 1, 2))
 
         def layer1(bank, b, a, g):
             cols = slice(P * (g % 4), P * (g % 4 + 1))
@@ -166,17 +165,17 @@ def tile_list_tabmlp_res_kernel(tc, tab, w1, w2_words, w2_scales, prev, offs, ou
 
         gather_words(0, 0)
         gather_words(0, 1)
-        gather_scales(0)
-        gather_scales(1)
-        quantize_w1(0, 0, 0)
         gather_words(1, 0)
         gather_words(1, 1)
+        gather_scales(0)
+        gather_scales(1)
+        quantize_w1(0, 0, 88)
+        quantize_w1(1, 0, 0)
         quantize_w1(0, 1, 88)
         quantize_w1(0, 2, 128)
         gather_words(2, 0, 256)
         gather_words(2, 1, 256)
         quantize_w1(1, 1, 0)
-        quantize_w1(1, 0, 128)
         quantize_w1(1, 2, 128)
 
         for b in range(HB):
@@ -188,19 +187,23 @@ def tile_list_tabmlp_res_kernel(tc, tab, w1, w2_words, w2_scales, prev, offs, ou
 
         for b in range(HB):
             banks = [psum.tile([P, 4, P], F32, name=f"bank{g}") for g in range(BANKS)]
-            early = KA - 1 if b == 0 else 0
-            for a in passes[b][:early]:
-                for g in range(BANKS):
+            ahead = BANKS if b == 0 else BANKS // 2
+            for a in range(KA - 1):
+                for g in range(ahead):
                     layer1(banks[g], b, a, g)
             for g in range(BANKS):
                 bank = banks[g]
-                for a in passes[b][early:]:
+                for a in range(KA - 1 if g < ahead else 0, KA):
                     layer1(bank, b, a, g)
-                rectify(bank, b, g, b == HB - 1 and g % 2 == 1)
+                rectify(bank, b, g, False)
                 if b == 0 and g == BANKS - 1:
                     quantize_h(b, 0, S)
-                if b == 1 and g % 2 == 1:
-                    quantize_h(b, P * (g - 1), 2 * P)
+                if b == 1 and g == 3:
+                    quantize_h(b, 0, 4 * P)
+                if b == 1 and g == 5:
+                    quantize_h(b, 4 * P, 2 * P)
+                if b == 1 and g > 5:
+                    quantize_h(b, P * g, P)
 
         results = [keep.tile([P, S], F32, name=f"result_{n}") for n in range(NT)]
         turns = [(n, s) for s in range(NS) for n in range(2)]

@@ -34,13 +34,10 @@ def tile_list_tabmlp_res_kernel(tc, tab, w1, w2_words, w2_scales, prev, offs, ou
         offsets = keep.tile([P, S // 16], U16, name="offsets")
         nc.sync.dma_start(offsets[:], offs)
 
-        tab_scales = keep.tile([P, T // 4], I32, name="tab_scales", align_bytes=64)
+        tab_scales = keep.tile([P, T // 4], I32, name="tab_scales", align_bytes=256)
         nc.vector.memset(tab_scales[:], 0)
-        w2_planes = keep.tile([P, HB, M // 4], I32, name="w2_planes", align_bytes=64)
+        w2_planes = keep.tile([P, HB, M // 4], I32, name="w2_planes", align_bytes=256)
         nc.vector.memset(w2_planes[:], 0)
-        warm = keep.tile([P, 1], F32, name="warm")
-        nc.vector.memset(warm[:], 0.0)
-        nc.scalar.activation(warm[:], warm[:], RELU)
 
         tab_bytes = tab[:, PASS * T :].rearrange("a (q t) -> a q t", t=T)
 
@@ -48,13 +45,13 @@ def tile_list_tabmlp_res_kernel(tc, tab, w1, w2_words, w2_scales, prev, offs, ou
         w1_raw = {}
 
         def load_tab(a):
-            tab_words[a] = keep.tile([P, T], I32, name=f"tab_words_{a}", align_bytes=64)
+            tab_words[a] = keep.tile([P, T], I32, name=f"tab_words_{a}", align_bytes=256)
             nc.sync.dma_start(
                 tab_words[a][:], tab[a, 0 : PASS * T].rearrange("(p x) -> p x", p=P).bitcast(I32)
             )
 
         def load_w1(first, a, count=1):
-            raw = keep.tile([P, 4, count * PASS], F32, name=f"w1_raw_{first}_{a}")
+            raw = keep.tile([P, 4, count * PASS], F32, name=f"w1_raw_{first}_{a}", align_bytes=256)
             nc.sync.dma_start(
                 raw[:],
                 w1[PASS * a : PASS * (a + 1), PASS * first : PASS * (first + count)].rearrange(
@@ -65,18 +62,19 @@ def tile_list_tabmlp_res_kernel(tc, tab, w1, w2_words, w2_scales, prev, offs, ou
                 w1_raw[first + i, a] = raw[:, :, PASS * i : PASS * (i + 1)]
 
         load_tab(0)
-        load_tab(1)
+        load_w1(0, 0)
         for q in range(4):
             nc.sync.dma_start(
                 tab_scales[32 * q : 32 * q + 4 * KA, :],
                 tab_bytes[:, 4 * q : 4 * q + 4, :].bitcast(I32),
             )
-        load_w1(0, 0, HB)
+        load_tab(1)
         load_w1(0, 1, HB)
         load_w1(0, 2)
         load_tab(2)
+        load_w1(1, 0)
         load_w1(1, 2)
-        w2_codes = keep.tile([P, HB, M // 2], I32, name="w2_codes", align_bytes=64)
+        w2_codes = keep.tile([P, HB, M // 2], I32, name="w2_codes", align_bytes=256)
         nc.sync.dma_start(w2_codes[:], w2_words.rearrange("b p x -> p b x").bitcast(I32))
         for r in range(4):
             nc.sync.dma_start(
@@ -85,37 +83,41 @@ def tile_list_tabmlp_res_kernel(tc, tab, w1, w2_words, w2_scales, prev, offs, ou
             )
         prev_sb = []
         for u in range(NT // 2):
-            prev_sb.append(keep.tile([P, 2, S], F32, name=f"prev_{u}"))
+            prev_sb.append(keep.tile([P, 2, S], F32, name=f"prev_{u}", align_bytes=256))
             nc.sync.dma_start(prev_sb[u][:], prev[256 * u : 256 * (u + 1), :].rearrange("(t p) j -> p t j", p=P))
 
         w1_codes = {}
         w1_planes = {}
 
-        reused = {(1, 1): "tab_words_2"}
+        reused = {(0, 0): "tab_scales", (1, 1): "tab_words_2"}
+        w1_grouped = {}
 
-        def quantize_w1(b, a, on_vector):
-            grouped = keep.tile([P, 4, P, 4], BF16, name=f"grouped_{b}_{a}", align_bytes=64)
+        def lay_out_w1(b, a, on_vector):
+            grouped = keep.tile([P, 4, P, 4], BF16, name="w1_raw_0_2" if (b, a) == (1, 1) else f"grouped_{b}_{a}", align_bytes=256)
+            w1_grouped[b, a] = grouped
             src = w1_raw[b, a].rearrange("p j (m t) -> p m j t", t=4)
             dst = grouped[:].rearrange("p t m j -> p m j t")
             if on_vector < P:
                 nc.scalar.copy(dst[:, on_vector:P], src[:, on_vector:P])
             if on_vector > 0:
                 nc.vector.tensor_copy(dst[:, 0:on_vector], src[:, 0:on_vector])
+
+        def quantize_w1(b, a):
             w1_codes[b, a] = keep.tile(
-                [P, PASS], U32, name=reused.get((b, a), f"w1_codes_{b}_{a}"), align_bytes=64
+                [P, PASS], U32, name=reused.get((b, a), f"w1_codes_{b}_{a}"), align_bytes=256
             )
-            w1_planes[b, a] = keep.tile([P, PASS], U8, name=f"w1_planes_{b}_{a}", align_bytes=64)
+            w1_planes[b, a] = keep.tile([P, PASS], U8, name=f"w1_planes_{b}_{a}", align_bytes=256)
             nc.vector.quantize_mx(
                 out=w1_codes[b, a][:].bitcast(FP8X4),
                 scales=w1_planes[b, a][:],
-                in_=grouped[:].rearrange("p t m j -> p (t m j)"),
+                in_=w1_grouped[b, a][:].rearrange("p t m j -> p (t m j)"),
             )
 
         picked = {}
         picked_scales = {}
 
         def gather_words(a, s, n=512):
-            picked[a, s] = keep.tile([P, 512], U32, name=f"picked_{a}_{s}", align_bytes=64)
+            picked[a, s] = keep.tile([P, 512], U32, name=f"picked_{a}_{s}", align_bytes=256)
             for c0 in range(0, 512, n):
                 first = (512 * s + c0) // 16
                 nc.vector.tensor_copy(
@@ -124,13 +126,13 @@ def tile_list_tabmlp_res_kernel(tc, tab, w1, w2_words, w2_scales, prev, offs, ou
                 )
 
         def gather_scales(s):
-            picked_scales[s] = keep.tile([P, 512], U8, name=f"picked_scales_{s}", align_bytes=64)
+            picked_scales[s] = keep.tile([P, 512], U8, name=f"picked_scales_{s}", align_bytes=256)
             nc.vector.tensor_copy(
                 picked_scales[s][:],
                 tab_scales[:].bitcast(U8).indirect(offsets[:, 32 * s : 32 * (s + 1)]),
             )
 
-        passes = ((0, 1, 2), (0, 1, 2))
+        passes = ((0, 1, 2), (1, 0, 2))
 
         def layer1(bank, b, a, g):
             cols = slice(P * (g % 4), P * (g % 4 + 1))
@@ -165,47 +167,56 @@ def tile_list_tabmlp_res_kernel(tc, tab, w1, w2_words, w2_scales, prev, offs, ou
 
         gather_words(0, 0)
         gather_words(0, 1)
-        gather_words(1, 0)
-        gather_words(1, 1)
         gather_scales(0)
         gather_scales(1)
-        quantize_w1(0, 0, 88)
-        quantize_w1(1, 0, 0)
-        quantize_w1(0, 1, 88)
-        quantize_w1(0, 2, 128)
+        lay_out_w1(0, 0, 0)
+        quantize_w1(0, 0)
+        gather_words(1, 0)
+        gather_words(1, 1)
+        lay_out_w1(0, 1, 88)
+        quantize_w1(0, 1)
+        lay_out_w1(0, 2, 88)
+        quantize_w1(0, 2)
+        lay_out_w1(1, 1, 0)
         gather_words(2, 0, 256)
         gather_words(2, 1, 256)
-        quantize_w1(1, 1, 0)
-        quantize_w1(1, 2, 128)
+        quantize_w1(1, 1)
+        lay_out_w1(1, 0, 128)
+        quantize_w1(1, 0)
+        lay_out_w1(1, 2, 128)
+        quantize_w1(1, 2)
 
         for b in range(HB):
-            h_grouped[b] = keep.tile([P, S, 4], BF16, name=f"h_grouped_{b}", align_bytes=64)
+            h_grouped[b] = keep.tile([P, S, 4], BF16, name=f"h_grouped_{b}", align_bytes=256)
             h_codes[b] = keep.tile(
-                [P, S], U32, name=f"grouped_{HB - 1}_{KA - 1}" if b == 0 else f"h_codes_{b}", align_bytes=64
+                [P, S], U32, name=f"grouped_1_2" if b == 0 else f"h_codes_{b}", align_bytes=256
             )
-            h_planes[b] = keep.tile([P, S], U8, name=f"h_planes_{b}", align_bytes=64)
+            h_planes[b] = keep.tile([P, S], U8, name=f"h_planes_{b}", align_bytes=256)
 
-        for b in range(HB):
-            banks = [psum.tile([P, 4, P], F32, name=f"bank{g}") for g in range(BANKS)]
-            ahead = BANKS if b == 0 else BANKS // 2
-            for a in range(KA - 1):
-                for g in range(ahead):
-                    layer1(banks[g], b, a, g)
+        banks = [psum.tile([P, 4, P], F32, name=f"bank{g}") for g in range(BANKS)]
+        for a in range(KA):
             for g in range(BANKS):
-                bank = banks[g]
-                for a in range(KA - 1 if g < ahead else 0, KA):
-                    layer1(bank, b, a, g)
-                rectify(bank, b, g, False)
-                if b == 0 and g == BANKS - 1:
-                    quantize_h(b, 0, S)
-                if b == 1 and g == 3:
-                    quantize_h(b, 0, 4 * P)
-                if b == 1 and g == 5:
-                    quantize_h(b, 4 * P, 2 * P)
-                if b == 1 and g > 5:
-                    quantize_h(b, P * g, P)
+                layer1(banks[g], 0, a, g)
+                if a == KA - 1:
+                    rectify(banks[g], 0, g, False)
+        quantize_h(0, 0, S)
 
-        results = [keep.tile([P, S], F32, name=f"result_{n}") for n in range(NT)]
+        banks = [psum.tile([P, 4, P], F32, name=f"bank{g}") for g in range(BANKS)]
+        for g in range(BANKS):
+            layer1(banks[g], 1, 1, g)
+        for g in range(5):
+            layer1(banks[g], 1, 0, g)
+        for g in range(BANKS):
+            if g >= 5:
+                layer1(banks[g], 1, 0, g)
+            layer1(banks[g], 1, 2, g)
+            rectify(banks[g], 1, g, g in (2, 6))
+            if g == 3:
+                quantize_h(1, 0, 4 * P)
+            if g in (5, 7):
+                quantize_h(1, P * (g - 1), 2 * P)
+
+        results = [keep.tile([P, S], F32, name=f"result_{n}", align_bytes=256) for n in range(NT)]
         turns = [(n, s) for s in range(NS) for n in range(2)]
         turns.extend((n, s) for n in range(2, NT) for s in range(NS))
         for turn, (n, s) in enumerate(turns):
@@ -222,7 +233,7 @@ def tile_list_tabmlp_res_kernel(tc, tab, w1, w2_words, w2_scales, prev, offs, ou
                     stop=(b == HB - 1),
                 )
             nc.vector.tensor_tensor(results[n][:, cols], bank[:], prev_sb[n // 2][:, n % 2, cols], ADD)
-            if n < 2:
+            if n < 2 or n == NT - 1:
                 nc.sync.dma_start(out[P * n : P * (n + 1), cols], results[n][:, cols])
             elif s == NS - 1:
                 nc.sync.dma_start(out[P * n : P * (n + 1), :], results[n][:])

@@ -89,11 +89,11 @@ def tile_list_tabmlp_res_kernel(tc, tab, w1, w2_words, w2_scales, prev, offs, ou
         w1_codes = {}
         w1_planes = {}
 
-        reused = {(0, 0): "tab_scales", (1, 1): "tab_words_2"}
+        reused = {(0, 0): "tab_words_1"}
         w1_grouped = {}
 
         def lay_out_w1(b, a, on_vector):
-            grouped = keep.tile([P, 4, P, 4], BF16, name="w1_raw_0_2" if (b, a) == (1, 1) else f"grouped_{b}_{a}", align_bytes=256)
+            grouped = keep.tile([P, 4, P, 4], BF16, name=f"grouped_{b}_{a}", align_bytes=256)
             w1_grouped[b, a] = grouped
             src = w1_raw[b, a].rearrange("p j (m t) -> p m j t", t=4)
             dst = grouped[:].rearrange("p t m j -> p m j t")
@@ -170,17 +170,17 @@ def tile_list_tabmlp_res_kernel(tc, tab, w1, w2_words, w2_scales, prev, offs, ou
         gather_scales(0)
         gather_scales(1)
         lay_out_w1(0, 0, 0)
-        quantize_w1(0, 0)
         gather_words(1, 0)
         gather_words(1, 1)
+        quantize_w1(0, 0)
         lay_out_w1(0, 1, 88)
         quantize_w1(0, 1)
-        lay_out_w1(0, 2, 88)
+        lay_out_w1(1, 1, 56)
+        quantize_w1(1, 1)
+        lay_out_w1(0, 2, 64)
         quantize_w1(0, 2)
-        lay_out_w1(1, 1, 0)
         gather_words(2, 0, 256)
         gather_words(2, 1, 256)
-        quantize_w1(1, 1)
         lay_out_w1(1, 0, 128)
         quantize_w1(1, 0)
         lay_out_w1(1, 2, 128)
@@ -204,8 +204,9 @@ def tile_list_tabmlp_res_kernel(tc, tab, w1, w2_words, w2_scales, prev, offs, ou
         banks = [psum.tile([P, 4, P], F32, name=f"bank{g}") for g in range(BANKS)]
         for g in range(BANKS):
             layer1(banks[g], 1, 1, g)
-        for g in range(5):
-            layer1(banks[g], 1, 0, g)
+            if g >= 4:
+                layer1(banks[g - 4], 1, 0, g - 4)
+        layer1(banks[4], 1, 0, 4)
         for g in range(BANKS):
             if g >= 5:
                 layer1(banks[g], 1, 0, g)
@@ -213,8 +214,10 @@ def tile_list_tabmlp_res_kernel(tc, tab, w1, w2_words, w2_scales, prev, offs, ou
             rectify(banks[g], 1, g, g in (2, 6))
             if g == 3:
                 quantize_h(1, 0, 4 * P)
-            if g in (5, 7):
-                quantize_h(1, P * (g - 1), 2 * P)
+            if g == 5:
+                quantize_h(1, 4 * P, 2 * P)
+            if g > 5:
+                quantize_h(1, P * g, P)
 
         results = [keep.tile([P, S], F32, name=f"result_{n}", align_bytes=256) for n in range(NT)]
         turns = [(n, s) for s in range(NS) for n in range(2)]
@@ -233,7 +236,7 @@ def tile_list_tabmlp_res_kernel(tc, tab, w1, w2_words, w2_scales, prev, offs, ou
                     stop=(b == HB - 1),
                 )
             nc.vector.tensor_tensor(results[n][:, cols], bank[:], prev_sb[n // 2][:, n % 2, cols], ADD)
-            if n < 2 or n == NT - 1:
+            if n < 2:
                 nc.sync.dma_start(out[P * n : P * (n + 1), cols], results[n][:, cols])
             elif s == NS - 1:
                 nc.sync.dma_start(out[P * n : P * (n + 1), :], results[n][:])

@@ -32,7 +32,6 @@ def tile_list_tabmlp_res_kernel(tc, tab, w1, w2_words, w2_scales, prev, offs, ou
         psum = ctx.enter_context(tc.psum_pool(name="psum", bufs=1))
 
         offsets = keep.tile([P, S // 16], U16, name="offsets")
-        nc.sync.dma_start(offsets[:], offs)
 
         tab_scales = keep.tile([P, T // 4], I32, name="tab_scales", align_bytes=256)
         nc.vector.memset(tab_scales[:], 0)
@@ -62,17 +61,18 @@ def tile_list_tabmlp_res_kernel(tc, tab, w1, w2_words, w2_scales, prev, offs, ou
                 w1_raw[first + i, a] = raw[:, :, PASS * i : PASS * (i + 1)]
 
         load_tab(0)
-        load_w1(0, 0)
+        nc.sync.dma_start(offsets[:], offs)
+        load_w1(0, 1)
         for q in range(4):
             nc.sync.dma_start(
                 tab_scales[32 * q : 32 * q + 4 * KA, :],
                 tab_bytes[:, 4 * q : 4 * q + 4, :].bitcast(I32),
             )
         load_tab(1)
-        load_w1(0, 1, HB)
+        load_w1(0, 0, HB)
         load_w1(0, 2)
         load_tab(2)
-        load_w1(1, 0)
+        load_w1(1, 1)
         load_w1(1, 2)
         w2_codes = keep.tile([P, HB, M // 2], I32, name="w2_codes", align_bytes=256)
         nc.sync.dma_start(w2_codes[:], w2_words.rearrange("b p x -> p b x").bitcast(I32))
@@ -88,13 +88,13 @@ def tile_list_tabmlp_res_kernel(tc, tab, w1, w2_words, w2_scales, prev, offs, ou
 
         w1_codes = {}
         w1_planes = {}
-
-        reused = {(0, 0): "tab_words_1"}
         w1_grouped = {}
 
         def lay_out_w1(b, a, on_vector):
             grouped = keep.tile([P, 4, P, 4], BF16, name=f"grouped_{b}_{a}", align_bytes=256)
-            w1_grouped[b, a] = grouped
+            for u in range(2):
+                w1_grouped[b, a, u] = grouped[:, 2 * u : 2 * u + 2]
+            w1_grouped[b, a] = grouped[:]
             src = w1_raw[b, a].rearrange("p j (m t) -> p m j t", t=4)
             dst = grouped[:].rearrange("p t m j -> p m j t")
             if on_vector < P:
@@ -102,15 +102,36 @@ def tile_list_tabmlp_res_kernel(tc, tab, w1, w2_words, w2_scales, prev, offs, ou
             if on_vector > 0:
                 nc.vector.tensor_copy(dst[:, 0:on_vector], src[:, 0:on_vector])
 
+        def lay_out_half(b, a, u, on_vector):
+            grouped = keep.tile([P, 2, P, 4], BF16, name=f"grouped_{b}_{a}_{u}", align_bytes=256)
+            w1_grouped[b, a, u] = grouped[:]
+            src = w1_raw[b, a].rearrange("p j (m t) -> p m j t", t=4)[:, :, :, 2 * u : 2 * u + 2]
+            dst = grouped[:].rearrange("p t m j -> p m j t")
+            if on_vector:
+                nc.vector.tensor_copy(dst, src)
+            else:
+                nc.scalar.copy(dst, src)
+
+        def codes_of(b, a):
+            if (b, a) not in w1_codes:
+                w1_codes[b, a] = keep.tile([P, PASS], U32, name=f"w1_codes_{b}_{a}", align_bytes=256)
+                w1_planes[b, a] = keep.tile([P, PASS], U8, name=f"w1_planes_{b}_{a}", align_bytes=256)
+            return w1_codes[b, a], w1_planes[b, a]
+
         def quantize_w1(b, a):
-            w1_codes[b, a] = keep.tile(
-                [P, PASS], U32, name=reused.get((b, a), f"w1_codes_{b}_{a}"), align_bytes=256
-            )
-            w1_planes[b, a] = keep.tile([P, PASS], U8, name=f"w1_planes_{b}_{a}", align_bytes=256)
+            codes, planes = codes_of(b, a)
             nc.vector.quantize_mx(
-                out=w1_codes[b, a][:].bitcast(FP8X4),
-                scales=w1_planes[b, a][:],
-                in_=w1_grouped[b, a][:].rearrange("p t m j -> p (t m j)"),
+                out=codes[:].bitcast(FP8X4),
+                scales=planes[:],
+                in_=w1_grouped[b, a].rearrange("p t m j -> p (t m j)"),
+            )
+
+        def quantize_half(b, a, u):
+            codes, planes = codes_of(b, a)
+            nc.vector.quantize_mx(
+                out=codes[:, 256 * u : 256 * (u + 1)].bitcast(FP8X4),
+                scales=planes[:, 256 * u : 256 * (u + 1)],
+                in_=w1_grouped[b, a, u].rearrange("p t m j -> p (t m j)"),
             )
 
         picked = {}
@@ -132,11 +153,11 @@ def tile_list_tabmlp_res_kernel(tc, tab, w1, w2_words, w2_scales, prev, offs, ou
                 tab_scales[:].bitcast(U8).indirect(offsets[:, 32 * s : 32 * (s + 1)]),
             )
 
-        passes = ((0, 1, 2), (1, 0, 2))
+        passes = ((1, 0, 2), (0, 1, 2))
 
-        def layer1(bank, b, a, g):
+        def layer1(bank, b, a, g, js=range(4)):
             cols = slice(P * (g % 4), P * (g % 4 + 1))
-            for j in range(4):
+            for j in js:
                 nc.tensor.matmul_mx(
                     out=bank[:, j, :],
                     lhsT=w1_codes[b, a][:, P * j : P * (j + 1)].bitcast(FP8X4),
@@ -169,49 +190,58 @@ def tile_list_tabmlp_res_kernel(tc, tab, w1, w2_words, w2_scales, prev, offs, ou
         gather_words(0, 1)
         gather_scales(0)
         gather_scales(1)
-        lay_out_w1(0, 0, 0)
+        lay_out_w1(0, 1, 0)
+        quantize_w1(0, 1)
         gather_words(1, 0)
         gather_words(1, 1)
-        quantize_w1(0, 0)
-        lay_out_w1(0, 1, 88)
-        quantize_w1(0, 1)
-        lay_out_w1(1, 1, 56)
-        quantize_w1(1, 1)
-        lay_out_w1(0, 2, 64)
-        quantize_w1(0, 2)
+        lay_out_half(0, 0, 0, True)
+        quantize_half(0, 0, 0)
+        lay_out_w1(1, 0, 64)
+        lay_out_half(0, 0, 1, False)
+        quantize_w1(1, 0)
+        quantize_half(0, 0, 1)
+        lay_out_half(0, 2, 0, True)
+        lay_out_half(0, 2, 1, False)
+        quantize_half(0, 2, 0)
+        quantize_half(0, 2, 1)
         gather_words(2, 0, 256)
         gather_words(2, 1, 256)
-        lay_out_w1(1, 0, 128)
-        quantize_w1(1, 0)
-        lay_out_w1(1, 2, 128)
-        quantize_w1(1, 2)
+        for a in (1, 2):
+            for u in range(2):
+                lay_out_half(1, a, u, True)
+            for u in range(2):
+                quantize_half(1, a, u)
 
         for b in range(HB):
             h_grouped[b] = keep.tile([P, S, 4], BF16, name=f"h_grouped_{b}", align_bytes=256)
             h_codes[b] = keep.tile(
-                [P, S], U32, name=f"grouped_1_2" if b == 0 else f"h_codes_{b}", align_bytes=256
+                [P, S], U32, name="grouped_1_2_1" if b == 0 else f"h_codes_{b}", align_bytes=256
             )
             h_planes[b] = keep.tile([P, S], U8, name=f"h_planes_{b}", align_bytes=256)
 
         banks = [psum.tile([P, 4, P], F32, name=f"bank{g}") for g in range(BANKS)]
-        for a in range(KA):
+        for g in range(BANKS):
+            layer1(banks[g], 0, 1, g)
+        for u in range(2):
             for g in range(BANKS):
-                layer1(banks[g], 0, a, g)
-                if a == KA - 1:
-                    rectify(banks[g], 0, g, False)
+                layer1(banks[g], 0, 0, g, range(2 * u, 2 * u + 2))
+        for g in range(BANKS):
+            layer1(banks[g], 0, 2, g)
+            rectify(banks[g], 0, g, False)
         quantize_h(0, 0, S)
 
         banks = [psum.tile([P, 4, P], F32, name=f"bank{g}") for g in range(BANKS)]
         for g in range(BANKS):
-            layer1(banks[g], 1, 1, g)
+            layer1(banks[g], 1, 0, g)
             if g >= 4:
-                layer1(banks[g - 4], 1, 0, g - 4)
-        layer1(banks[4], 1, 0, 4)
+                layer1(banks[g - 4], 1, 1, g - 4)
+        for g in range(2):
+            layer1(banks[g], 1, 2, g, range(2))
         for g in range(BANKS):
-            if g >= 5:
-                layer1(banks[g], 1, 0, g)
-            layer1(banks[g], 1, 2, g)
-            rectify(banks[g], 1, g, g in (2, 6))
+            if g >= 4:
+                layer1(banks[g], 1, 1, g)
+            layer1(banks[g], 1, 2, g, range(2, 4) if g < 2 else range(4))
+            rectify(banks[g], 1, g, g == 2)
             if g == 3:
                 quantize_h(1, 0, 4 * P)
             if g == 5:
@@ -236,7 +266,7 @@ def tile_list_tabmlp_res_kernel(tc, tab, w1, w2_words, w2_scales, prev, offs, ou
                     stop=(b == HB - 1),
                 )
             nc.vector.tensor_tensor(results[n][:, cols], bank[:], prev_sb[n // 2][:, n % 2, cols], ADD)
-            if n < 2:
+            if n in (0, 1):
                 nc.sync.dma_start(out[P * n : P * (n + 1), cols], results[n][:, cols])
             elif s == NS - 1:
                 nc.sync.dma_start(out[P * n : P * (n + 1), :], results[n][:])

@@ -31,12 +31,17 @@ def tile_list_tabmlp_res_kernel(tc, tab, w1, w2_words, w2_scales, prev, offs, ou
         keep = ctx.enter_context(tc.tile_pool(name="keep", bufs=1))
         psum = ctx.enter_context(tc.psum_pool(name="psum", bufs=1))
 
+        def staggered(columns, dtype, size, shift, name):
+            padded = keep.tile([P, columns + shift // size], dtype, name=name, align_bytes=256)
+            return padded[:, shift // size :]
+
         offsets = keep.tile([P, S // 16], U16, name="offsets")
 
         tab_scales = keep.tile([P, T // 4], I32, name="tab_scales", align_bytes=256)
         nc.vector.memset(tab_scales[:], 0)
-        w2_planes = keep.tile([P, HB, M // 4], I32, name="w2_planes", align_bytes=256)
-        nc.vector.memset(w2_planes[:], 0)
+        w2_planes = staggered(HB * M // 4, I32, 4, 192, "w2_planes")
+        nc.vector.memset(w2_planes, 0)
+        w2_planes = w2_planes.rearrange("p (b x) -> p b x", b=HB)
 
         tab_bytes = tab[:, PASS * T :].rearrange("a (q t) -> a q t", t=T)
 
@@ -74,8 +79,8 @@ def tile_list_tabmlp_res_kernel(tc, tab, w1, w2_words, w2_scales, prev, offs, ou
         load_tab(2)
         load_w1(1, 1)
         load_w1(1, 2)
-        w2_codes = keep.tile([P, HB, M // 2], I32, name="w2_codes", align_bytes=256)
-        nc.sync.dma_start(w2_codes[:], w2_words.rearrange("b p x -> p b x").bitcast(I32))
+        w2_codes = staggered(HB * M // 2, I32, 4, 128, "w2_codes").rearrange("p (b x) -> p b x", b=HB)
+        nc.sync.dma_start(w2_codes, w2_words.rearrange("b p x -> p b x").bitcast(I32))
         for r in range(4):
             nc.sync.dma_start(
                 w2_planes[r:P:32, :, :],
@@ -114,15 +119,15 @@ def tile_list_tabmlp_res_kernel(tc, tab, w1, w2_words, w2_scales, prev, offs, ou
 
         def codes_of(b, a):
             if (b, a) not in w1_codes:
-                w1_codes[b, a] = keep.tile([P, PASS], U32, name=f"w1_codes_{b}_{a}", align_bytes=256)
-                w1_planes[b, a] = keep.tile([P, PASS], U8, name=f"w1_planes_{b}_{a}", align_bytes=256)
+                w1_codes[b, a] = staggered(PASS, U32, 4, 128, f"w1_codes_{b}_{a}")
+                w1_planes[b, a] = staggered(PASS, U8, 1, 192, f"w1_planes_{b}_{a}")
             return w1_codes[b, a], w1_planes[b, a]
 
         def quantize_w1(b, a):
             codes, planes = codes_of(b, a)
             nc.vector.quantize_mx(
-                out=codes[:].bitcast(FP8X4),
-                scales=planes[:],
+                out=codes.bitcast(FP8X4),
+                scales=planes,
                 in_=w1_grouped[b, a].rearrange("p t m j -> p (t m j)"),
             )
 
@@ -132,6 +137,13 @@ def tile_list_tabmlp_res_kernel(tc, tab, w1, w2_words, w2_scales, prev, offs, ou
                 out=codes[:, 256 * u : 256 * (u + 1)].bitcast(FP8X4),
                 scales=planes[:, 256 * u : 256 * (u + 1)],
                 in_=w1_grouped[b, a, u].rearrange("p t m j -> p (t m j)"),
+            )
+
+        def quantize_quarter(j, codes):
+            nc.vector.quantize_mx(
+                out=codes.bitcast(FP8X4),
+                scales=w1_planes[0, 0][:, P * j : P * (j + 1)],
+                in_=w1_grouped[0, 0, 1][:, j - 2].rearrange("p m j -> p (m j)"),
             )
 
         picked = {}
@@ -147,9 +159,9 @@ def tile_list_tabmlp_res_kernel(tc, tab, w1, w2_words, w2_scales, prev, offs, ou
                 )
 
         def gather_scales(s):
-            picked_scales[s] = keep.tile([P, 512], U8, name=f"picked_scales_{s}", align_bytes=256)
+            picked_scales[s] = staggered(512, U8, 1, 64, f"picked_scales_{s}")
             nc.vector.tensor_copy(
-                picked_scales[s][:],
+                picked_scales[s],
                 tab_scales[:].bitcast(U8).indirect(offsets[:, 32 * s : 32 * (s + 1)]),
             )
 
@@ -160,7 +172,7 @@ def tile_list_tabmlp_res_kernel(tc, tab, w1, w2_words, w2_scales, prev, offs, ou
             for j in js:
                 nc.tensor.matmul_mx(
                     out=bank[:, j, :],
-                    lhsT=w1_codes[b, a][:, P * j : P * (j + 1)].bitcast(FP8X4),
+                    lhsT=(held_codes if (b, a, j) == (0, 0, 3) else w1_codes[b, a][:, P * j : P * (j + 1)]).bitcast(FP8X4),
                     lhsT_scale=w1_planes[b, a][:, P * j : P * (j + 1)],
                     rhs=picked[a, g // 4][:, cols].bitcast(FP8X4),
                     rhs_scale=picked_scales[g // 4][4 * a : P, cols],
@@ -199,10 +211,12 @@ def tile_list_tabmlp_res_kernel(tc, tab, w1, w2_words, w2_scales, prev, offs, ou
         lay_out_w1(1, 0, 64)
         lay_out_half(0, 0, 1, False)
         quantize_w1(1, 0)
-        quantize_half(0, 0, 1)
+        quantize_quarter(2, w1_codes[0, 0][:, 2 * P : 3 * P])
         lay_out_half(0, 2, 0, True)
         lay_out_half(0, 2, 1, False)
         quantize_half(0, 2, 0)
+        held_codes = staggered(P, U32, 4, 128, "w1_raw_0_2")
+        quantize_quarter(3, held_codes)
         quantize_half(0, 2, 1)
         gather_words(2, 0, 256)
         gather_words(2, 1, 256)
@@ -217,14 +231,14 @@ def tile_list_tabmlp_res_kernel(tc, tab, w1, w2_words, w2_scales, prev, offs, ou
             h_codes[b] = keep.tile(
                 [P, S], U32, name="grouped_1_2_1" if b == 0 else f"h_codes_{b}", align_bytes=256
             )
-            h_planes[b] = keep.tile([P, S], U8, name=f"h_planes_{b}", align_bytes=256)
+            h_planes[b] = staggered(S, U8, 1, 64, f"h_planes_{b}")
 
         banks = [psum.tile([P, 4, P], F32, name=f"bank{g}") for g in range(BANKS)]
         for g in range(BANKS):
             layer1(banks[g], 0, 1, g)
-        for u in range(2):
+        for js in ((0, 1), (2,), (3,)):
             for g in range(BANKS):
-                layer1(banks[g], 0, 0, g, range(2 * u, 2 * u + 2))
+                layer1(banks[g], 0, 0, g, js)
         for g in range(BANKS):
             layer1(banks[g], 0, 2, g)
             rectify(banks[g], 0, g, False)

@@ -67,13 +67,13 @@ def tile_list_tabmlp_res_kernel(tc, tab, w1, w2_words, w2_scales, prev, offs, ou
 
         load_tab(0)
         nc.sync.dma_start(offsets[:], offs)
-        load_w1(0, 1)
+        load_tab(1)
         for q in range(4):
             nc.sync.dma_start(
                 tab_scales[32 * q : 32 * q + 4 * KA, :],
                 tab_bytes[:, 4 * q : 4 * q + 4, :].bitcast(I32),
             )
-        load_tab(1)
+        load_w1(0, 1)
         load_w1(0, 0, HB)
         load_w1(0, 2)
         load_tab(2)
@@ -143,7 +143,7 @@ def tile_list_tabmlp_res_kernel(tc, tab, w1, w2_words, w2_scales, prev, offs, ou
             nc.vector.quantize_mx(
                 out=codes.bitcast(FP8X4),
                 scales=w1_planes[0, 0][:, P * j : P * (j + 1)],
-                in_=w1_grouped[0, 0, 1][:, j - 2].rearrange("p m j -> p (m j)"),
+                in_=w1_grouped[0, 0, j // 2][:, j % 2].rearrange("p m j -> p (m j)"),
             )
 
         picked = {}
@@ -200,16 +200,20 @@ def tile_list_tabmlp_res_kernel(tc, tab, w1, w2_words, w2_scales, prev, offs, ou
 
         gather_words(0, 0)
         gather_words(0, 1)
-        gather_scales(0)
-        gather_scales(1)
-        lay_out_w1(0, 1, 0)
-        quantize_w1(0, 1)
         gather_words(1, 0)
         gather_words(1, 1)
+        gather_scales(0)
+        gather_scales(1)
+        lay_out_half(0, 1, 0, True)
+        lay_out_half(0, 1, 1, False)
+        quantize_half(0, 1, 0)
+        quantize_half(0, 1, 1)
         lay_out_half(0, 0, 0, True)
-        quantize_half(0, 0, 0)
+        codes_of(0, 0)
+        quantize_quarter(0, w1_codes[0, 0][:, 0:P])
         lay_out_w1(1, 0, 64)
         lay_out_half(0, 0, 1, False)
+        quantize_quarter(1, w1_codes[0, 0][:, P : 2 * P])
         quantize_w1(1, 0)
         quantize_quarter(2, w1_codes[0, 0][:, 2 * P : 3 * P])
         lay_out_half(0, 2, 0, True)
@@ -236,7 +240,7 @@ def tile_list_tabmlp_res_kernel(tc, tab, w1, w2_words, w2_scales, prev, offs, ou
         banks = [psum.tile([P, 4, P], F32, name=f"bank{g}") for g in range(BANKS)]
         for g in range(BANKS):
             layer1(banks[g], 0, 1, g)
-        for js in ((0, 1), (2,), (3,)):
+        for js in ((0,), (1,), (2,), (3,)):
             for g in range(BANKS):
                 layer1(banks[g], 0, 0, g, js)
         for g in range(BANKS):
@@ -260,14 +264,16 @@ def tile_list_tabmlp_res_kernel(tc, tab, w1, w2_words, w2_scales, prev, offs, ou
                 quantize_h(1, 0, 4 * P)
             if g == 5:
                 quantize_h(1, 4 * P, 2 * P)
-            if g > 5:
+            if g == 6:
                 quantize_h(1, P * g, P)
 
         results = [keep.tile([P, S], F32, name=f"result_{n}", align_bytes=256) for n in range(NT)]
-        turns = [(n, s) for s in range(NS) for n in range(2)]
-        turns.extend((n, s) for n in range(2, NT) for s in range(NS))
+        turns = [(n, s) for s in range(NS) for n in range(3)]
+        turns.extend((n, s) for n in range(3, NT) for s in range(NS))
         for turn, (n, s) in enumerate(turns):
             cols = slice(512 * s, 512 * (s + 1))
+            if turn == 1:
+                quantize_h(1, 7 * P, P)
             bank = psum.tile([P, 512], F32, name=f"bank{turn % BANKS}")
             for b in range(HB):
                 nc.tensor.matmul_mx(
@@ -279,7 +285,11 @@ def tile_list_tabmlp_res_kernel(tc, tab, w1, w2_words, w2_scales, prev, offs, ou
                     start=(b == 0),
                     stop=(b == HB - 1),
                 )
-            nc.vector.tensor_tensor(results[n][:, cols], bank[:], prev_sb[n // 2][:, n % 2, cols], ADD)
+            if turn in (2,):
+                nc.scalar.copy(results[n][:, cols], bank[:])
+                nc.gpsimd.tensor_tensor(results[n][:, cols], results[n][:, cols], prev_sb[n // 2][:, n % 2, cols], ADD)
+            else:
+                nc.vector.tensor_tensor(results[n][:, cols], bank[:], prev_sb[n // 2][:, n % 2, cols], ADD)
             if n in (0, 1):
                 nc.sync.dma_start(out[P * n : P * (n + 1), cols], results[n][:, cols])
             elif s == NS - 1:

@@ -268,6 +268,7 @@ def tile_list_tabmlp_res_kernel(tc, tab, w1, w2_words, w2_scales, prev, offs, ou
                 quantize_h(1, P * g, P)
 
         results = [keep.tile([P, S], F32, name=f"result_{n}", align_bytes=256) for n in range(NT)]
+        queues = (nc.scalar, nc.sync)
         turns = [(n, s) for s in range(NS) for n in range(3)]
         turns.extend((n, s) for n in range(3, NT) for s in range(NS))
         for turn, (n, s) in enumerate(turns):
@@ -291,6 +292,6 @@ def tile_list_tabmlp_res_kernel(tc, tab, w1, w2_words, w2_scales, prev, offs, ou
             else:
                 nc.vector.tensor_tensor(results[n][:, cols], bank[:], prev_sb[n // 2][:, n % 2, cols], ADD)
             if n in (0, 1):
-                nc.sync.dma_start(out[P * n : P * (n + 1), cols], results[n][:, cols])
+                queues[n % 2].dma_start(out[P * n : P * (n + 1), cols], results[n][:, cols])
             elif s == NS - 1:
-                nc.sync.dma_start(out[P * n : P * (n + 1), :], results[n][:])
+                queues[n % 2].dma_start(out[P * n : P * (n + 1), :], results[n][:])

@@ -20,9 +20,12 @@ P = 128
 PASS = 512
 KA = K // PASS
 HB = H // PASS
-NS = S // 512
+SIDE = 512
+SIDES = S // SIDE
 NT = M // P
 BANKS = 8
+STORE_RUNS = (3, 3, 2)
+GPSIMD_TURNS = (3, 8)
 
 
 def tile_list_tabmlp_res_kernel(tc, tab, w1, w2_words, w2_scales, prev, offs, out):
@@ -36,13 +39,11 @@ def tile_list_tabmlp_res_kernel(tc, tab, w1, w2_words, w2_scales, prev, offs, ou
             return padded[:, shift // size :]
 
         offsets = keep.tile([P, S // 16], U16, name="offsets")
-
         tab_scales = keep.tile([P, T // 4], I32, name="tab_scales", align_bytes=256)
         nc.vector.memset(tab_scales[:], 0)
         w2_planes = staggered(HB * M // 4, I32, 4, 192, "w2_planes")
         nc.vector.memset(w2_planes, 0)
         w2_planes = w2_planes.rearrange("p (b x) -> p b x", b=HB)
-
         tab_bytes = tab[:, PASS * T :].rearrange("a (q t) -> a q t", t=T)
 
         tab_words = {}
@@ -50,248 +51,201 @@ def tile_list_tabmlp_res_kernel(tc, tab, w1, w2_words, w2_scales, prev, offs, ou
 
         def load_tab(a):
             tab_words[a] = keep.tile([P, T], I32, name=f"tab_words_{a}", align_bytes=256)
-            nc.sync.dma_start(
-                tab_words[a][:], tab[a, 0 : PASS * T].rearrange("(p x) -> p x", p=P).bitcast(I32)
-            )
+            nc.sync.dma_start(tab_words[a][:], tab[a, 0 : PASS * T].rearrange("(p x) -> p x", p=P).bitcast(I32))
 
-        def load_w1(first, a, count=1):
-            raw = keep.tile([P, 4, count * PASS], F32, name=f"w1_raw_{first}_{a}", align_bytes=256)
+        def load_w1(b, a):
+            w1_raw[b, a] = keep.tile([P, 4, PASS], F32, name=f"w1_raw_{b}_{a}", align_bytes=256)
             nc.sync.dma_start(
-                raw[:],
-                w1[PASS * a : PASS * (a + 1), PASS * first : PASS * (first + count)].rearrange(
-                    "(p j) c -> p j c", j=4
-                ),
+                w1_raw[b, a][:],
+                w1[PASS * a : PASS * (a + 1), PASS * b : PASS * (b + 1)].rearrange("(p j) c -> p j c", j=4),
             )
-            for i in range(count):
-                w1_raw[first + i, a] = raw[:, :, PASS * i : PASS * (i + 1)]
 
         load_tab(0)
         nc.sync.dma_start(offsets[:], offs)
-        load_tab(1)
+        load_w1(0, 0)
         for q in range(4):
             nc.sync.dma_start(
                 tab_scales[32 * q : 32 * q + 4 * KA, :],
                 tab_bytes[:, 4 * q : 4 * q + 4, :].bitcast(I32),
             )
-        load_w1(0, 1)
-        load_w1(0, 0, HB)
-        load_w1(0, 2)
-        load_tab(2)
-        load_w1(1, 1)
-        load_w1(1, 2)
-        w2_codes = staggered(HB * M // 2, I32, 4, 128, "w2_codes").rearrange("p (b x) -> p b x", b=HB)
-        nc.sync.dma_start(w2_codes, w2_words.rearrange("b p x -> p b x").bitcast(I32))
         for r in range(4):
             nc.sync.dma_start(
                 w2_planes[r:P:32, :, :],
                 w2_scales[:, r:16:4, :].rearrange("b q n -> q b n").bitcast(I32),
             )
+        for a in range(1, KA):
+            load_w1(0, a)
+            load_tab(a)
+        for a in range(KA):
+            load_w1(1, a)
+        w2_codes = staggered(HB * M // 2, I32, 4, 128, "w2_codes").rearrange("p (b x) -> p b x", b=HB)
+        nc.sync.dma_start(w2_codes, w2_words.rearrange("b p x -> p b x").bitcast(I32))
         prev_sb = []
-        for u in range(NT // 2):
-            prev_sb.append(keep.tile([P, 2, S], F32, name=f"prev_{u}", align_bytes=256))
-            nc.sync.dma_start(prev_sb[u][:], prev[256 * u : 256 * (u + 1), :].rearrange("(t p) j -> p t j", p=P))
+        for s in range(SIDES):
+            prev_sb.append(keep.tile([P, NT, SIDE], F32, name=f"prev_{s}", align_bytes=256))
+            nc.sync.dma_start(prev_sb[s][:], prev[:, SIDE * s : SIDE * (s + 1)].rearrange("(t p) j -> p t j", p=P))
 
         w1_codes = {}
         w1_planes = {}
         w1_grouped = {}
 
-        def lay_out_w1(b, a, on_vector):
-            grouped = keep.tile([P, 4, P, 4], BF16, name=f"grouped_{b}_{a}", align_bytes=256)
-            for u in range(2):
-                w1_grouped[b, a, u] = grouped[:, 2 * u : 2 * u + 2]
-            w1_grouped[b, a] = grouped[:]
-            src = w1_raw[b, a].rearrange("p j (m t) -> p m j t", t=4)
-            dst = grouped[:].rearrange("p t m j -> p m j t")
-            if on_vector < P:
-                nc.scalar.copy(dst[:, on_vector:P], src[:, on_vector:P])
-            if on_vector > 0:
-                nc.vector.tensor_copy(dst[:, 0:on_vector], src[:, 0:on_vector])
-
-        def lay_out_half(b, a, u, on_vector):
+        def lay_out(b, a, u, on_scalar):
             grouped = keep.tile([P, 2, P, 4], BF16, name=f"grouped_{b}_{a}_{u}", align_bytes=256)
             w1_grouped[b, a, u] = grouped[:]
-            src = w1_raw[b, a].rearrange("p j (m t) -> p m j t", t=4)[:, :, :, 2 * u : 2 * u + 2]
+            src = w1_raw[b, a][:].rearrange("p j (m t) -> p m j t", t=4)[:, :, :, 2 * u : 2 * u + 2]
             dst = grouped[:].rearrange("p t m j -> p m j t")
-            if on_vector:
-                nc.vector.tensor_copy(dst, src)
-            else:
-                nc.scalar.copy(dst, src)
+            if on_scalar > 0:
+                nc.scalar.copy(dst[:, 0:on_scalar], src[:, 0:on_scalar])
+            if on_scalar < P:
+                nc.vector.tensor_copy(dst[:, on_scalar:P], src[:, on_scalar:P])
 
-        def codes_of(b, a):
-            if (b, a) not in w1_codes:
-                w1_codes[b, a] = staggered(PASS, U32, 4, 128, f"w1_codes_{b}_{a}")
-                w1_planes[b, a] = staggered(PASS, U8, 1, 192, f"w1_planes_{b}_{a}")
-            return w1_codes[b, a], w1_planes[b, a]
-
-        def quantize_w1(b, a):
-            codes, planes = codes_of(b, a)
+        def quantize_w1(b, a, u):
+            w1_codes[b, a, u] = staggered(2 * P, U32, 4, 128, f"w1_codes_{b}_{a}_{u}")
+            w1_planes[b, a, u] = staggered(2 * P, U8, 1, 192, f"w1_planes_{b}_{a}_{u}")
             nc.vector.quantize_mx(
-                out=codes.bitcast(FP8X4),
-                scales=planes,
-                in_=w1_grouped[b, a].rearrange("p t m j -> p (t m j)"),
-            )
-
-        def quantize_half(b, a, u):
-            codes, planes = codes_of(b, a)
-            nc.vector.quantize_mx(
-                out=codes[:, 256 * u : 256 * (u + 1)].bitcast(FP8X4),
-                scales=planes[:, 256 * u : 256 * (u + 1)],
+                out=w1_codes[b, a, u].bitcast(FP8X4),
+                scales=w1_planes[b, a, u],
                 in_=w1_grouped[b, a, u].rearrange("p t m j -> p (t m j)"),
             )
 
-        def quantize_quarter(j, codes):
-            nc.vector.quantize_mx(
-                out=codes.bitcast(FP8X4),
-                scales=w1_planes[0, 0][:, P * j : P * (j + 1)],
-                in_=w1_grouped[0, 0, j // 2][:, j % 2].rearrange("p m j -> p (m j)"),
-            )
+        def prepare_w1(b, a, on_scalar):
+            lay_out(b, a, 0, 0)
+            lay_out(b, a, 1, on_scalar)
+            quantize_w1(b, a, 0)
+            quantize_w1(b, a, 1)
 
         picked = {}
         picked_scales = {}
 
-        def gather_words(a, s, n=512):
-            picked[a, s] = keep.tile([P, 512], U32, name=f"picked_{a}_{s}", align_bytes=256)
-            for c0 in range(0, 512, n):
-                first = (512 * s + c0) // 16
+        def gather_words(a, s, n):
+            picked[a, s] = keep.tile([P, SIDE], U32, name=f"picked_{a}_{s}", align_bytes=256)
+            for c0 in range(0, SIDE, n):
+                first = (SIDE * s + c0) // 16
                 nc.vector.tensor_copy(
                     picked[a, s][:, c0 : c0 + n],
                     tab_words[a][:].bitcast(U32).indirect(offsets[:, first : first + n // 16]),
                 )
 
         def gather_scales(s):
-            picked_scales[s] = staggered(512, U8, 1, 64, f"picked_scales_{s}")
+            picked_scales[s] = staggered(SIDE, U8, 1, 64, f"picked_scales_{s}")
             nc.vector.tensor_copy(
                 picked_scales[s],
                 tab_scales[:].bitcast(U8).indirect(offsets[:, 32 * s : 32 * (s + 1)]),
             )
 
-        passes = ((1, 0, 2), (0, 1, 2))
-
-        def layer1(bank, b, a, g, js=range(4)):
+        def layer1(bank, b, a, g, js, last=KA - 1):
             cols = slice(P * (g % 4), P * (g % 4 + 1))
             for j in js:
+                part = slice(P * (j % 2), P * (j % 2 + 1))
                 nc.tensor.matmul_mx(
                     out=bank[:, j, :],
-                    lhsT=(held_codes if (b, a, j) == (0, 0, 3) else w1_codes[b, a][:, P * j : P * (j + 1)]).bitcast(FP8X4),
-                    lhsT_scale=w1_planes[b, a][:, P * j : P * (j + 1)],
+                    lhsT=w1_codes[b, a, j // 2][:, part].bitcast(FP8X4),
+                    lhsT_scale=w1_planes[b, a, j // 2][:, part],
                     rhs=picked[a, g // 4][:, cols].bitcast(FP8X4),
                     rhs_scale=picked_scales[g // 4][4 * a : P, cols],
-                    start=(a == passes[b][0] and j == 0),
-                    stop=(a == passes[b][-1] and j == 3),
+                    start=(a == 0 and j == 0),
+                    stop=(a == last and j == 3),
                 )
 
         h_grouped = {}
         h_codes = {}
         h_planes = {}
-        def quantize_h(b, c0, n):
-            nc.vector.quantize_mx(
-                out=h_codes[b][:, c0 : c0 + n].bitcast(FP8X4),
-                scales=h_planes[b][:, c0 : c0 + n],
-                in_=h_grouped[b][:, c0 : c0 + n, :].rearrange("p n j -> p (n j)"),
-            )
 
         def rectify(bank, b, g, on_vector):
-            dst = h_grouped[b][:, P * g : P * (g + 1), :]
+            if g % 4 == 0:
+                h_grouped[b, g // 4] = keep.tile([P, SIDE, 4], BF16, name=f"h_grouped_{b}_{g // 4}", align_bytes=256)
+            dst = h_grouped[b, g // 4][:, P * (g % 4) : P * (g % 4 + 1), :]
             src = bank[:].rearrange("p j n -> p n j")
             if on_vector:
                 nc.vector.tensor_scalar_max(dst, src, 0.0)
             else:
                 nc.scalar.activation(dst, src, RELU)
 
-        gather_words(0, 0)
-        gather_words(0, 1)
-        gather_words(1, 0)
-        gather_words(1, 1)
-        gather_scales(0)
-        gather_scales(1)
-        lay_out_half(0, 1, 0, True)
-        lay_out_half(0, 1, 1, False)
-        quantize_half(0, 1, 0)
-        quantize_half(0, 1, 1)
-        lay_out_half(0, 0, 0, True)
-        codes_of(0, 0)
-        quantize_quarter(0, w1_codes[0, 0][:, 0:P])
-        lay_out_w1(1, 0, 64)
-        lay_out_half(0, 0, 1, False)
-        quantize_quarter(1, w1_codes[0, 0][:, P : 2 * P])
-        quantize_w1(1, 0)
-        quantize_quarter(2, w1_codes[0, 0][:, 2 * P : 3 * P])
-        lay_out_half(0, 2, 0, True)
-        lay_out_half(0, 2, 1, False)
-        quantize_half(0, 2, 0)
-        held_codes = staggered(P, U32, 4, 128, "w1_raw_0_2")
-        quantize_quarter(3, held_codes)
-        quantize_half(0, 2, 1)
-        gather_words(2, 0, 256)
-        gather_words(2, 1, 256)
-        for a in (1, 2):
-            for u in range(2):
-                lay_out_half(1, a, u, True)
-            for u in range(2):
-                quantize_half(1, a, u)
-
-        for b in range(HB):
-            h_grouped[b] = keep.tile([P, S, 4], BF16, name=f"h_grouped_{b}", align_bytes=256)
-            h_codes[b] = keep.tile(
-                [P, S], U32, name="grouped_1_2_1" if b == 0 else f"h_codes_{b}", align_bytes=256
+        def quantize_h(b, s, codes, first=0, count=4):
+            if first == 0:
+                h_codes[b, s] = codes
+                h_planes[b, s] = staggered(SIDE, U8, 1, 64, f"h_planes_{b}_{s}")
+            cols = slice(P * first, P * (first + count))
+            nc.vector.quantize_mx(
+                out=codes[:, cols].bitcast(FP8X4),
+                scales=h_planes[b, s][:, cols],
+                in_=h_grouped[b, s][:, cols, :].rearrange("p n j -> p (n j)"),
             )
-            h_planes[b] = staggered(S, U8, 1, 64, f"h_planes_{b}")
 
         banks = [psum.tile([P, 4, P], F32, name=f"bank{g}") for g in range(BANKS)]
-        for g in range(BANKS):
-            layer1(banks[g], 0, 1, g)
-        for js in ((0,), (1,), (2,), (3,)):
-            for g in range(BANKS):
-                layer1(banks[g], 0, 0, g, js)
-        for g in range(BANKS):
-            layer1(banks[g], 0, 2, g)
-            rectify(banks[g], 0, g, False)
-        quantize_h(0, 0, S)
+        for s in range(SIDES):
+            gather_words(0, s, SIDE)
+        prepare_w1(0, 0, P)
+        for s in range(SIDES):
+            gather_scales(s)
+            for g in range(4 * s, 4 * s + 4):
+                layer1(banks[g], 0, 0, g, range(4))
+        for a in range(1, KA):
+            prepare_w1(0, a, P)
+            for s in range(SIDES):
+                gather_words(a, s, SIDE if a < KA - 1 else SIDE // 2)
+                for g in range(4 * s, 4 * s + 4):
+                    layer1(banks[g], 0, a, g, range(4))
+                    if a == KA - 1:
+                        rectify(banks[g], 0, g, False)
 
         banks = [psum.tile([P, 4, P], F32, name=f"bank{g}") for g in range(BANKS)]
-        for g in range(BANKS):
-            layer1(banks[g], 1, 0, g)
-            if g >= 4:
-                layer1(banks[g - 4], 1, 1, g - 4)
-        for g in range(2):
+        prepare_w1(1, 0, 0)
+        for g in range(BANKS - 1):
+            layer1(banks[g], 1, 0, g, range(4))
+        prepare_w1(1, 1, 0)
+        for g in range(4):
+            layer1(banks[g], 1, 1, g, range(4))
+        layer1(banks[BANKS - 1], 1, 0, BANKS - 1, range(4))
+        prepare_w1(1, 2, P)
+        held = keep.tile([P, S], U32, name="grouped_1_2_1", align_bytes=256)
+        for s in range(SIDES):
+            quantize_h(0, s, held[:, SIDE * s : SIDE * (s + 1)])
+        h_last = keep.tile([P, S], U32, name="h_last", align_bytes=256)
+        for g in range(4):
             layer1(banks[g], 1, 2, g, range(2))
-        for g in range(BANKS):
-            if g >= 4:
-                layer1(banks[g], 1, 1, g)
-            layer1(banks[g], 1, 2, g, range(2, 4) if g < 2 else range(4))
-            rectify(banks[g], 1, g, g == 2)
-            if g == 3:
-                quantize_h(1, 0, 4 * P)
+        for g in range(4):
+            layer1(banks[g], 1, 2, g, range(2, 4))
+            rectify(banks[g], 1, g, g % 2 == 1)
+        quantize_h(1, 0, h_last[:, 0:SIDE])
+        for g in range(4, BANKS):
+            layer1(banks[g], 1, 2, g, range(4), 1)
+            layer1(banks[g], 1, 1, g, range(4), 1)
+            rectify(banks[g], 1, g, False)
             if g == 5:
-                quantize_h(1, 4 * P, 2 * P)
+                quantize_h(1, 1, h_last[:, SIDE:S], 0, 2)
             if g == 6:
-                quantize_h(1, P * g, P)
+                quantize_h(1, 1, h_last[:, SIDE:S], 2, 1)
 
-        results = [keep.tile([P, S], F32, name=f"result_{n}", align_bytes=256) for n in range(NT)]
-        queues = (nc.scalar, nc.sync)
-        turns = [(n, s) for s in range(NS) for n in range(3)]
-        turns.extend((n, s) for n in range(3, NT) for s in range(NS))
-        for turn, (n, s) in enumerate(turns):
-            cols = slice(512 * s, 512 * (s + 1))
-            if turn == 1:
-                quantize_h(1, 7 * P, P)
-            bank = psum.tile([P, 512], F32, name=f"bank{turn % BANKS}")
-            for b in range(HB):
-                nc.tensor.matmul_mx(
-                    out=bank[:],
-                    lhsT=w2_codes[:, b, :].bitcast(U8)[:, 256 * n : 256 * (n + 1)].bitcast(FP4X4),
-                    lhsT_scale=w2_planes[:, b, :].bitcast(U8)[:, P * n : P * (n + 1)],
-                    rhs=h_codes[b][:, cols].bitcast(FP8X4),
-                    rhs_scale=h_planes[b][:, cols],
-                    start=(b == 0),
-                    stop=(b == HB - 1),
+        dead_slots = [f"w1_raw_0_{a}" for a in range(KA)] + [f"tab_words_{a}" for a in range(KA)]
+        turn = 0
+        for s in range(SIDES):
+            cols = slice(SIDE * s, SIDE * (s + 1))
+            first = 0
+            for run in STORE_RUNS:
+                result = keep.tile([P, run, SIDE], F32, name=dead_slots.pop(), align_bytes=256)
+                for n in range(first, first + run):
+                    bank = psum.tile([P, SIDE], F32, name=f"bank{turn % BANKS}")
+                    for b in range(HB):
+                        nc.tensor.matmul_mx(
+                            out=bank[:],
+                            lhsT=w2_codes[:, b, :].bitcast(U8)[:, 256 * n : 256 * (n + 1)].bitcast(FP4X4),
+                            lhsT_scale=w2_planes[:, b, :].bitcast(U8)[:, P * n : P * (n + 1)],
+                            rhs=h_codes[b, s].bitcast(FP8X4),
+                            rhs_scale=h_planes[b, s],
+                            start=(b == 0),
+                            stop=(b == HB - 1),
+                        )
+                    total = result[:, n - first, :]
+                    if turn in GPSIMD_TURNS:
+                        nc.scalar.copy(total, bank[:])
+                        nc.gpsimd.tensor_tensor(total, total, prev_sb[s][:, n, :], ADD)
+                    else:
+                        nc.vector.tensor_tensor(total, bank[:], prev_sb[s][:, n, :], ADD)
+                    if turn == 0:
+                        quantize_h(1, 1, h_last[:, SIDE:S], 3, 1)
+                    turn += 1
+                nc.sync.dma_start(
+                    out[P * first : P * (first + run), cols].rearrange("(t p) j -> p t j", p=P), result[:]
                 )
-            if turn in (2,):
-                nc.scalar.copy(results[n][:, cols], bank[:])
-                nc.gpsimd.tensor_tensor(results[n][:, cols], results[n][:, cols], prev_sb[n // 2][:, n % 2, cols], ADD)
-            else:
-                nc.vector.tensor_tensor(results[n][:, cols], bank[:], prev_sb[n // 2][:, n % 2, cols], ADD)
-            if n in (0, 1):
-                queues[n % 2].dma_start(out[P * n : P * (n + 1), cols], results[n][:, cols])
-            elif s == NS - 1:
-                queues[n % 2].dma_start(out[P * n : P * (n + 1), :], results[n][:])
+                first += run

@@ -24,8 +24,9 @@ SIDE = 512
 SIDES = S // SIDE
 NT = M // P
 BANKS = 8
-STORE_RUNS = (3, 3, 2)
-GPSIMD_TURNS = (3, 8)
+STORE_TILES = 2
+PREV_TILES = 4
+GPSIMD_TURNS = (0, 8)
 
 
 def tile_list_tabmlp_res_kernel(tc, tab, w1, w2_words, w2_scales, prev, offs, out):
@@ -68,11 +69,6 @@ def tile_list_tabmlp_res_kernel(tc, tab, w1, w2_words, w2_scales, prev, offs, ou
                 tab_scales[32 * q : 32 * q + 4 * KA, :],
                 tab_bytes[:, 4 * q : 4 * q + 4, :].bitcast(I32),
             )
-        for r in range(4):
-            nc.sync.dma_start(
-                w2_planes[r:P:32, :, :],
-                w2_scales[:, r:16:4, :].rearrange("b q n -> q b n").bitcast(I32),
-            )
         for a in range(1, KA):
             load_w1(0, a)
             load_tab(a)
@@ -80,10 +76,16 @@ def tile_list_tabmlp_res_kernel(tc, tab, w1, w2_words, w2_scales, prev, offs, ou
             load_w1(1, a)
         w2_codes = staggered(HB * M // 2, I32, 4, 128, "w2_codes").rearrange("p (b x) -> p b x", b=HB)
         nc.sync.dma_start(w2_codes, w2_words.rearrange("b p x -> p b x").bitcast(I32))
+        for r in range(4):
+            nc.sync.dma_start(
+                w2_planes[r:P:32, :, :],
+                w2_scales[:, r:16:4, :].rearrange("b q n -> q b n").bitcast(I32),
+            )
         prev_sb = []
-        for s in range(SIDES):
-            prev_sb.append(keep.tile([P, NT, SIDE], F32, name=f"prev_{s}", align_bytes=256))
-            nc.sync.dma_start(prev_sb[s][:], prev[:, SIDE * s : SIDE * (s + 1)].rearrange("(t p) j -> p t j", p=P))
+        for u in range(NT // PREV_TILES):
+            prev_sb.append(keep.tile([P, PREV_TILES, S], F32, name=f"prev_{u}", align_bytes=256))
+            rows = slice(P * PREV_TILES * u, P * PREV_TILES * (u + 1))
+            nc.sync.dma_start(prev_sb[u][:], prev[rows, :].rearrange("(t p) j -> p t j", p=P))
 
         w1_codes = {}
         w1_planes = {}
@@ -217,14 +219,15 @@ def tile_list_tabmlp_res_kernel(tc, tab, w1, w2_words, w2_scales, prev, offs, ou
             if g == 6:
                 quantize_h(1, 1, h_last[:, SIDE:S], 2, 1)
 
-        dead_slots = [f"w1_raw_0_{a}" for a in range(KA)] + [f"tab_words_{a}" for a in range(KA)]
+        dead_slots = [f"w1_raw_0_{a}" for a in range(KA)] + ["tab_words_0"]
+        queues = (nc.sync, nc.sync, nc.sync, nc.scalar)
         turn = 0
-        for s in range(SIDES):
-            cols = slice(SIDE * s, SIDE * (s + 1))
-            first = 0
-            for run in STORE_RUNS:
-                result = keep.tile([P, run, SIDE], F32, name=dead_slots.pop(), align_bytes=256)
-                for n in range(first, first + run):
+        for u in range(NT // STORE_TILES):
+            first = STORE_TILES * u
+            result = keep.tile([P, STORE_TILES, S], F32, name=dead_slots[u], align_bytes=256)
+            for s in range(SIDES):
+                cols = slice(SIDE * s, SIDE * (s + 1))
+                for n in range(first, first + STORE_TILES):
                     bank = psum.tile([P, SIDE], F32, name=f"bank{turn % BANKS}")
                     for b in range(HB):
                         nc.tensor.matmul_mx(
@@ -236,16 +239,15 @@ def tile_list_tabmlp_res_kernel(tc, tab, w1, w2_words, w2_scales, prev, offs, ou
                             start=(b == 0),
                             stop=(b == HB - 1),
                         )
-                    total = result[:, n - first, :]
+                    total = result[:, n - first, cols]
+                    before = prev_sb[n // PREV_TILES][:, n % PREV_TILES, cols]
                     if turn in GPSIMD_TURNS:
                         nc.scalar.copy(total, bank[:])
-                        nc.gpsimd.tensor_tensor(total, total, prev_sb[s][:, n, :], ADD)
+                        nc.gpsimd.tensor_tensor(total, total, before, ADD)
                     else:
-                        nc.vector.tensor_tensor(total, bank[:], prev_sb[s][:, n, :], ADD)
+                        nc.vector.tensor_tensor(total, bank[:], before, ADD)
                     if turn == 0:
                         quantize_h(1, 1, h_last[:, SIDE:S], 3, 1)
                     turn += 1
-                nc.sync.dma_start(
-                    out[P * first : P * (first + run), cols].rearrange("(t p) j -> p t j", p=P), result[:]
-                )
-                first += run
+            rows = slice(P * first, P * (first + STORE_TILES))
+            queues[u].dma_start(out[rows, :].rearrange("(t p) j -> p t j", p=P), result[:])

@@ -24,9 +24,9 @@ SIDE = 512
 SIDES = S // SIDE
 NT = M // P
 BANKS = 8
-STORE_TILES = 2
+EARLY_BANKS = 4
 PREV_TILES = 4
-GPSIMD_TURNS = (0, 8)
+GPSIMD_TURNS = ()
 
 
 def tile_list_tabmlp_res_kernel(tc, tab, w1, w2_words, w2_scales, prev, offs, out):
@@ -102,7 +102,8 @@ def tile_list_tabmlp_res_kernel(tc, tab, w1, w2_words, w2_scales, prev, offs, ou
                 nc.vector.tensor_copy(dst[:, on_scalar:P], src[:, on_scalar:P])
 
         def quantize_w1(b, a, u):
-            w1_codes[b, a, u] = staggered(2 * P, U32, 4, 128, f"w1_codes_{b}_{a}_{u}")
+            slot = "w1_raw_0_2" if (b, a, u) == (0, 1, 1) else f"w1_codes_{b}_{a}_{u}"
+            w1_codes[b, a, u] = staggered(2 * P, U32, 4, 128, slot)
             w1_planes[b, a, u] = staggered(2 * P, U8, 1, 192, f"w1_planes_{b}_{a}_{u}")
             nc.vector.quantize_mx(
                 out=w1_codes[b, a, u].bitcast(FP8X4),
@@ -182,27 +183,40 @@ def tile_list_tabmlp_res_kernel(tc, tab, w1, w2_words, w2_scales, prev, offs, ou
             gather_scales(s)
             for g in range(4 * s, 4 * s + 4):
                 layer1(banks[g], 0, 0, g, range(4))
-        for a in range(1, KA):
-            prepare_w1(0, a, P)
-            for s in range(SIDES):
-                gather_words(a, s, SIDE if a < KA - 1 else SIDE // 2)
-                for g in range(4 * s, 4 * s + 4):
-                    layer1(banks[g], 0, a, g, range(4))
-                    if a == KA - 1:
-                        rectify(banks[g], 0, g, False)
+        lay_out(0, 1, 0, 0)
+        lay_out(0, 1, 1, P)
+        quantize_w1(0, 1, 0)
+        for s in range(SIDES):
+            gather_words(1, s, SIDE)
+            for g in range(4 * s, 4 * s + 4):
+                layer1(banks[g], 0, 1, g, range(2))
+        lay_out(0, 2, 0, 0)
+        lay_out(0, 2, 1, P)
+        quantize_w1(0, 2, 0)
+        quantize_w1(0, 1, 1)
+        quantize_w1(0, 2, 1)
+        for g in range(BANKS):
+            layer1(banks[g], 0, 1, g, range(2, 4))
+        for s in range(SIDES):
+            gather_words(2, s, SIDE // 2)
+            for g in range(4 * s, 4 * s + 4):
+                layer1(banks[g], 0, 2, g, range(4))
+                rectify(banks[g], 0, g, False)
 
         banks = [psum.tile([P, 4, P], F32, name=f"bank{g}") for g in range(BANKS)]
         prepare_w1(1, 0, 0)
-        for g in range(BANKS - 1):
-            layer1(banks[g], 1, 0, g, range(4))
+        for g in range(3):
+            layer1(banks[g], 1, 0, g, range(2))
+        for g in range(BANKS):
+            layer1(banks[g], 1, 0, g, range(2, 4) if g < 3 else range(4))
         prepare_w1(1, 1, 0)
-        for g in range(4):
-            layer1(banks[g], 1, 1, g, range(4))
-        layer1(banks[BANKS - 1], 1, 0, BANKS - 1, range(4))
+        for g in range(3):
+            layer1(banks[g], 1, 1, g, range(2))
+        for g in range(EARLY_BANKS):
+            layer1(banks[g], 1, 1, g, range(2, 4) if g < 3 else range(4))
         prepare_w1(1, 2, P)
-        held = keep.tile([P, S], U32, name="grouped_1_2_1", align_bytes=256)
-        for s in range(SIDES):
-            quantize_h(0, s, held[:, SIDE * s : SIDE * (s + 1)])
+        held = keep.tile([P, SIDE], U32, name="grouped_1_2_1", align_bytes=256)
+        quantize_h(0, 0, held[:])
         h_last = keep.tile([P, S], U32, name="h_last", align_bytes=256)
         for g in range(4):
             layer1(banks[g], 1, 2, g, range(2))
@@ -210,44 +224,52 @@ def tile_list_tabmlp_res_kernel(tc, tab, w1, w2_words, w2_scales, prev, offs, ou
             layer1(banks[g], 1, 2, g, range(2, 4))
             rectify(banks[g], 1, g, g % 2 == 1)
         quantize_h(1, 0, h_last[:, 0:SIDE])
+        held = keep.tile([P, SIDE], U32, name="h_grouped_1_0", align_bytes=256)
+        quantize_h(0, 1, held[:])
         for g in range(4, BANKS):
-            layer1(banks[g], 1, 2, g, range(4), 1)
-            layer1(banks[g], 1, 1, g, range(4), 1)
+            if g < EARLY_BANKS:
+                layer1(banks[g], 1, 2, g, range(4))
+            else:
+                layer1(banks[g], 1, 2, g, range(4), 1)
+                layer1(banks[g], 1, 1, g, range(4), 1)
             rectify(banks[g], 1, g, False)
             if g == 5:
                 quantize_h(1, 1, h_last[:, SIDE:S], 0, 2)
             if g == 6:
                 quantize_h(1, 1, h_last[:, SIDE:S], 2, 1)
 
-        dead_slots = [f"w1_raw_0_{a}" for a in range(KA)] + ["tab_words_0"]
-        queues = (nc.sync, nc.sync, nc.sync, nc.scalar)
+        dead_slots = [f"w1_raw_0_{a}" for a in range(KA)] + [f"tab_words_{a}" for a in range(KA)] + ["w1_raw_1_0", "w1_raw_1_1"]
+        stores = [[(n, s) for n in range(2)] for s in range(SIDES)]
+        stores.extend([(n, s) for s in range(SIDES)] for n in range(2, NT))
         turn = 0
-        for u in range(NT // STORE_TILES):
-            first = STORE_TILES * u
-            result = keep.tile([P, STORE_TILES, S], F32, name=dead_slots[u], align_bytes=256)
-            for s in range(SIDES):
+        for u, sums in enumerate(stores):
+            result = keep.tile([P, 2, SIDE], F32, name=dead_slots[u], align_bytes=256)
+            for i, (n, s) in enumerate(sums):
                 cols = slice(SIDE * s, SIDE * (s + 1))
-                for n in range(first, first + STORE_TILES):
-                    bank = psum.tile([P, SIDE], F32, name=f"bank{turn % BANKS}")
-                    for b in range(HB):
-                        nc.tensor.matmul_mx(
-                            out=bank[:],
-                            lhsT=w2_codes[:, b, :].bitcast(U8)[:, 256 * n : 256 * (n + 1)].bitcast(FP4X4),
-                            lhsT_scale=w2_planes[:, b, :].bitcast(U8)[:, P * n : P * (n + 1)],
-                            rhs=h_codes[b, s].bitcast(FP8X4),
-                            rhs_scale=h_planes[b, s],
-                            start=(b == 0),
-                            stop=(b == HB - 1),
-                        )
-                    total = result[:, n - first, cols]
-                    before = prev_sb[n // PREV_TILES][:, n % PREV_TILES, cols]
-                    if turn in GPSIMD_TURNS:
-                        nc.scalar.copy(total, bank[:])
-                        nc.gpsimd.tensor_tensor(total, total, before, ADD)
-                    else:
-                        nc.vector.tensor_tensor(total, bank[:], before, ADD)
-                    if turn == 0:
-                        quantize_h(1, 1, h_last[:, SIDE:S], 3, 1)
-                    turn += 1
-            rows = slice(P * first, P * (first + STORE_TILES))
-            queues[u].dma_start(out[rows, :].rearrange("(t p) j -> p t j", p=P), result[:])
+                bank = psum.tile([P, SIDE], F32, name=f"bank{turn % BANKS}")
+                for b in range(HB):
+                    nc.tensor.matmul_mx(
+                        out=bank[:],
+                        lhsT=w2_codes[:, b, :].bitcast(U8)[:, 256 * n : 256 * (n + 1)].bitcast(FP4X4),
+                        lhsT_scale=w2_planes[:, b, :].bitcast(U8)[:, P * n : P * (n + 1)],
+                        rhs=h_codes[b, s].bitcast(FP8X4),
+                        rhs_scale=h_planes[b, s],
+                        start=(b == 0),
+                        stop=(b == HB - 1),
+                    )
+                total = result[:, i, :]
+                before = prev_sb[n // PREV_TILES][:, n % PREV_TILES, cols]
+                if turn in GPSIMD_TURNS:
+                    nc.scalar.copy(total, bank[:])
+                    nc.gpsimd.tensor_tensor(total, total, before, ADD)
+                else:
+                    nc.vector.tensor_tensor(total, bank[:], before, ADD)
+                if turn == 0:
+                    quantize_h(1, 1, h_last[:, SIDE:S], 3, 1)
+                turn += 1
+            if u < SIDES:
+                target = out[0 : 2 * P, SIDE * u : SIDE * (u + 1)].rearrange("(t p) j -> p t j", p=P)
+            else:
+                target = out[P * u : P * (u + 1), :].rearrange("p (s j) -> p s j", s=SIDES)
+            queue = nc.scalar if u == NT - 1 else nc.sync
+            queue.dma_start(target, result[:])

@@ -66,7 +66,7 @@ def tile_list_tabmlp_res_kernel(tc, tab, w1, w2_words, w2_scales, prev, offs, ou
         load_w1(0, 0)
         for q in range(4):
             nc.sync.dma_start(
-                tab_scales[32 * q : 32 * q + 4 * KA, :],
+                tab_scales[32 * q + 4 : 32 * q + 4 + 4 * KA, :],
                 tab_bytes[:, 4 * q : 4 * q + 4, :].bitcast(I32),
             )
         for a in range(1, KA):
@@ -136,19 +136,20 @@ def tile_list_tabmlp_res_kernel(tc, tab, w1, w2_words, w2_scales, prev, offs, ou
                 tab_scales[:].bitcast(U8).indirect(offsets[:, 32 * s : 32 * (s + 1)]),
             )
 
-        def layer1(bank, b, a, g, js, last=KA - 1):
-            cols = slice(P * (g % 4), P * (g % 4 + 1))
+        def layer1(banks, b, a, gs, js, last=KA - 1):
             for j in js:
                 part = slice(P * (j % 2), P * (j % 2 + 1))
-                nc.tensor.matmul_mx(
-                    out=bank[:, j, :],
-                    lhsT=w1_codes[b, a, j // 2][:, part].bitcast(FP8X4),
-                    lhsT_scale=w1_planes[b, a, j // 2][:, part],
-                    rhs=picked[a, g // 4][:, cols].bitcast(FP8X4),
-                    rhs_scale=picked_scales[g // 4][4 * a : P, cols],
-                    start=(a == 0 and j == 0),
-                    stop=(a == last and j == 3),
-                )
+                for g in gs:
+                    cols = slice(P * (g % 4), P * (g % 4 + 1))
+                    nc.tensor.matmul_mx(
+                        out=banks[g][:, j, :],
+                        lhsT=w1_codes[b, a, j // 2][:, part].bitcast(FP8X4),
+                        lhsT_scale=w1_planes[b, a, j // 2][:, part],
+                        rhs=picked[a, g // 4][:, cols].bitcast(FP8X4),
+                        rhs_scale=picked_scales[g // 4][4 * (a + 1) : P, cols],
+                        start=(a == 0 and j == 0),
+                        stop=(a == last and j == 3),
+                    )
 
         h_grouped = {}
         h_codes = {}
@@ -181,62 +182,53 @@ def tile_list_tabmlp_res_kernel(tc, tab, w1, w2_words, w2_scales, prev, offs, ou
         prepare_w1(0, 0, P)
         for s in range(SIDES):
             gather_scales(s)
-            for g in range(4 * s, 4 * s + 4):
-                layer1(banks[g], 0, 0, g, range(4))
+            layer1(banks, 0, 0, range(4 * s, 4 * s + 4), range(4))
         lay_out(0, 1, 0, 0)
         lay_out(0, 1, 1, P)
         quantize_w1(0, 1, 0)
         for s in range(SIDES):
             gather_words(1, s, SIDE)
-            for g in range(4 * s, 4 * s + 4):
-                layer1(banks[g], 0, 1, g, range(2))
+            layer1(banks, 0, 1, range(4 * s, 4 * s + 4), range(2))
         lay_out(0, 2, 0, 0)
         lay_out(0, 2, 1, P)
         quantize_w1(0, 2, 0)
         quantize_w1(0, 1, 1)
         quantize_w1(0, 2, 1)
-        for g in range(BANKS):
-            layer1(banks[g], 0, 1, g, range(2, 4))
+        layer1(banks, 0, 1, range(BANKS), range(2, 4))
         for s in range(SIDES):
             gather_words(2, s, SIDE // 2)
-            for g in range(4 * s, 4 * s + 4):
-                layer1(banks[g], 0, 2, g, range(4))
+            for g in range(4 * s, 4 * s + 4, 2):
+                layer1(banks, 0, 2, (g, g + 1), range(4))
                 rectify(banks[g], 0, g, False)
+                rectify(banks[g + 1], 0, g + 1, False)
 
         banks = [psum.tile([P, 4, P], F32, name=f"bank{g}") for g in range(BANKS)]
         prepare_w1(1, 0, 0)
-        for g in range(3):
-            layer1(banks[g], 1, 0, g, range(2))
-        for g in range(BANKS):
-            layer1(banks[g], 1, 0, g, range(2, 4) if g < 3 else range(4))
+        for g in range(0, BANKS, 2):
+            layer1(banks, 1, 0, (g, g + 1), range(4))
         prepare_w1(1, 1, 0)
-        for g in range(3):
-            layer1(banks[g], 1, 1, g, range(2))
-        for g in range(EARLY_BANKS):
-            layer1(banks[g], 1, 1, g, range(2, 4) if g < 3 else range(4))
+        layer1(banks, 1, 1, range(EARLY_BANKS), range(4))
         prepare_w1(1, 2, P)
         held = keep.tile([P, SIDE], U32, name="grouped_1_2_1", align_bytes=256)
         quantize_h(0, 0, held[:])
         h_last = keep.tile([P, S], U32, name="h_last", align_bytes=256)
-        for g in range(4):
-            layer1(banks[g], 1, 2, g, range(2))
-        for g in range(4):
-            layer1(banks[g], 1, 2, g, range(2, 4))
-            rectify(banks[g], 1, g, g % 2 == 1)
+        layer1(banks, 1, 2, range(4), range(2))
+        for g in range(0, 4, 2):
+            layer1(banks, 1, 2, (g, g + 1), range(2, 4))
+            rectify(banks[g], 1, g, False)
+            rectify(banks[g + 1], 1, g + 1, True)
         quantize_h(1, 0, h_last[:, 0:SIDE])
         held = keep.tile([P, SIDE], U32, name="h_grouped_1_0", align_bytes=256)
         quantize_h(0, 1, held[:])
-        for g in range(4, BANKS):
-            if g < EARLY_BANKS:
-                layer1(banks[g], 1, 2, g, range(4))
-            else:
-                layer1(banks[g], 1, 2, g, range(4), 1)
-                layer1(banks[g], 1, 1, g, range(4), 1)
+        for g in range(4, BANKS, 2):
+            layer1(banks, 1, 2, (g, g + 1), range(4), 1)
+            layer1(banks, 1, 1, (g, g + 1), range(4), 1)
             rectify(banks[g], 1, g, False)
-            if g == 5:
-                quantize_h(1, 1, h_last[:, SIDE:S], 0, 2)
             if g == 6:
                 quantize_h(1, 1, h_last[:, SIDE:S], 2, 1)
+            rectify(banks[g + 1], 1, g + 1, False)
+            if g == 4:
+                quantize_h(1, 1, h_last[:, SIDE:S], 0, 2)
 
         dead_slots = [f"w1_raw_0_{a}" for a in range(KA)] + [f"tab_words_{a}" for a in range(KA)] + ["w1_raw_1_0", "w1_raw_1_1"]
         stores = [[(n, s) for n in range(2)] for s in range(SIDES)]

@@ -24,9 +24,7 @@ SIDE = 512
 SIDES = S // SIDE
 NT = M // P
 BANKS = 8
-EARLY_BANKS = 4
 PREV_TILES = 4
-GPSIMD_TURNS = ()
 
 
 def tile_list_tabmlp_res_kernel(tc, tab, w1, w2_words, w2_scales, prev, offs, out):
@@ -136,20 +134,29 @@ def tile_list_tabmlp_res_kernel(tc, tab, w1, w2_words, w2_scales, prev, offs, ou
                 tab_scales[:].bitcast(U8).indirect(offsets[:, 32 * s : 32 * (s + 1)]),
             )
 
-        def layer1(banks, b, a, gs, js, last=KA - 1):
-            for j in js:
+        passes_done = {}
+
+        def layer1(banks, b, a, order):
+            for g, j in order:
+                cols = slice(P * (g % 4), P * (g % 4 + 1))
                 part = slice(P * (j % 2), P * (j % 2 + 1))
-                for g in gs:
-                    cols = slice(P * (g % 4), P * (g % 4 + 1))
-                    nc.tensor.matmul_mx(
-                        out=banks[g][:, j, :],
-                        lhsT=w1_codes[b, a, j // 2][:, part].bitcast(FP8X4),
-                        lhsT_scale=w1_planes[b, a, j // 2][:, part],
-                        rhs=picked[a, g // 4][:, cols].bitcast(FP8X4),
-                        rhs_scale=picked_scales[g // 4][4 * (a + 1) : P, cols],
-                        start=(a == 0 and j == 0),
-                        stop=(a == last and j == 3),
-                    )
+                done = passes_done.get((b, g), 0)
+                passes_done[b, g] = done + 1
+                nc.tensor.matmul_mx(
+                    out=banks[g][:, j, :],
+                    lhsT=w1_codes[b, a, j // 2][:, part].bitcast(FP8X4),
+                    lhsT_scale=w1_planes[b, a, j // 2][:, part],
+                    rhs=picked[a, g // 4][:, cols].bitcast(FP8X4),
+                    rhs_scale=picked_scales[g // 4][4 * (a + 1) : P, cols],
+                    start=(done == 0),
+                    stop=(done == 4 * KA - 1),
+                )
+
+        def across(gs, js):
+            return [(g, j) for j in js for g in gs]
+
+        def within(g, js):
+            return [(g, j) for j in (js if g % 2 == 0 else reversed(js))]
 
         h_grouped = {}
         h_codes = {}
@@ -182,53 +189,52 @@ def tile_list_tabmlp_res_kernel(tc, tab, w1, w2_words, w2_scales, prev, offs, ou
         prepare_w1(0, 0, P)
         for s in range(SIDES):
             gather_scales(s)
-            layer1(banks, 0, 0, range(4 * s, 4 * s + 4), range(4))
-        lay_out(0, 1, 0, 0)
+            layer1(banks, 0, 0, across(range(4 * s, 4 * s + 4), range(4)))
+        lay_out(0, 1, 0, P)
         lay_out(0, 1, 1, P)
         quantize_w1(0, 1, 0)
         for s in range(SIDES):
             gather_words(1, s, SIDE)
-            layer1(banks, 0, 1, range(4 * s, 4 * s + 4), range(2))
+            layer1(banks, 0, 1, across(range(4 * s, 4 * s + 4), range(2)))
         lay_out(0, 2, 0, 0)
         lay_out(0, 2, 1, P)
         quantize_w1(0, 2, 0)
         quantize_w1(0, 1, 1)
         quantize_w1(0, 2, 1)
-        layer1(banks, 0, 1, range(BANKS), range(2, 4))
+        layer1(banks, 0, 1, across(range(BANKS), range(2, 4)))
         for s in range(SIDES):
             gather_words(2, s, SIDE // 2)
-            for g in range(4 * s, 4 * s + 4, 2):
-                layer1(banks, 0, 2, (g, g + 1), range(4))
+            for g in range(4 * s, 4 * s + 4):
+                layer1(banks, 0, 2, within(g, range(4)))
                 rectify(banks[g], 0, g, False)
-                rectify(banks[g + 1], 0, g + 1, False)
 
         banks = [psum.tile([P, 4, P], F32, name=f"bank{g}") for g in range(BANKS)]
         prepare_w1(1, 0, 0)
-        for g in range(0, BANKS, 2):
-            layer1(banks, 1, 0, (g, g + 1), range(4))
+        layer1(banks, 1, 0, across(range(3), range(2)))
+        layer1(banks, 1, 0, across(range(3), range(2, 4)))
+        for g in range(3, BANKS):
+            layer1(banks, 1, 0, within(g, range(4)))
         prepare_w1(1, 1, 0)
-        layer1(banks, 1, 1, range(EARLY_BANKS), range(4))
+        layer1(banks, 1, 1, across(range(4), range(4)))
         prepare_w1(1, 2, P)
         held = keep.tile([P, SIDE], U32, name="grouped_1_2_1", align_bytes=256)
         quantize_h(0, 0, held[:])
         h_last = keep.tile([P, S], U32, name="h_last", align_bytes=256)
-        layer1(banks, 1, 2, range(4), range(2))
-        for g in range(0, 4, 2):
-            layer1(banks, 1, 2, (g, g + 1), range(2, 4))
-            rectify(banks[g], 1, g, False)
-            rectify(banks[g + 1], 1, g + 1, True)
+        layer1(banks, 1, 2, across(range(4), range(2)))
+        for g in range(4):
+            layer1(banks, 1, 2, within(g, range(2, 4)))
+            rectify(banks[g], 1, g, g % 2 == 1)
         quantize_h(1, 0, h_last[:, 0:SIDE])
         held = keep.tile([P, SIDE], U32, name="h_grouped_1_0", align_bytes=256)
         quantize_h(0, 1, held[:])
-        for g in range(4, BANKS, 2):
-            layer1(banks, 1, 2, (g, g + 1), range(4), 1)
-            layer1(banks, 1, 1, (g, g + 1), range(4), 1)
+        for g in range(4, BANKS):
+            for a in (2, 1):
+                layer1(banks, 1, a, within(g, range(4)))
             rectify(banks[g], 1, g, False)
+            if g == 5:
+                quantize_h(1, 1, h_last[:, SIDE:S], 0, 2)
             if g == 6:
                 quantize_h(1, 1, h_last[:, SIDE:S], 2, 1)
-            rectify(banks[g + 1], 1, g + 1, False)
-            if g == 4:
-                quantize_h(1, 1, h_last[:, SIDE:S], 0, 2)
 
         dead_slots = [f"w1_raw_0_{a}" for a in range(KA)] + [f"tab_words_{a}" for a in range(KA)] + ["w1_raw_1_0", "w1_raw_1_1"]
         stores = [[(n, s) for n in range(2)] for s in range(SIDES)]
@@ -249,13 +255,8 @@ def tile_list_tabmlp_res_kernel(tc, tab, w1, w2_words, w2_scales, prev, offs, ou
                         start=(b == 0),
                         stop=(b == HB - 1),
                     )
-                total = result[:, i, :]
                 before = prev_sb[n // PREV_TILES][:, n % PREV_TILES, cols]
-                if turn in GPSIMD_TURNS:
-                    nc.scalar.copy(total, bank[:])
-                    nc.gpsimd.tensor_tensor(total, total, before, ADD)
-                else:
-                    nc.vector.tensor_tensor(total, bank[:], before, ADD)
+                nc.vector.tensor_tensor(result[:, i, :], bank[:], before, ADD)
                 if turn == 0:
                     quantize_h(1, 1, h_last[:, SIDE:S], 3, 1)
                 turn += 1

@@ -24,7 +24,7 @@ SIDE = 512
 SIDES = S // SIDE
 NT = M // P
 BANKS = 8
-PREV_TILES = 4
+PREV_RUNS = (2, 3, 3)
 
 
 def tile_list_tabmlp_res_kernel(tc, tab, w1, w2_words, w2_scales, prev, offs, out):
@@ -80,10 +80,11 @@ def tile_list_tabmlp_res_kernel(tc, tab, w1, w2_words, w2_scales, prev, offs, ou
                 w2_scales[:, r:16:4, :].rearrange("b q n -> q b n").bitcast(I32),
             )
         prev_sb = []
-        for u in range(NT // PREV_TILES):
-            prev_sb.append(keep.tile([P, PREV_TILES, S], F32, name=f"prev_{u}", align_bytes=256))
-            rows = slice(P * PREV_TILES * u, P * PREV_TILES * (u + 1))
-            nc.sync.dma_start(prev_sb[u][:], prev[rows, :].rearrange("(t p) j -> p t j", p=P))
+        for u, count in enumerate(PREV_RUNS):
+            run = keep.tile([P, count, S], F32, name=f"prev_{u}", align_bytes=256)
+            rows = slice(P * len(prev_sb), P * (len(prev_sb) + count))
+            nc.sync.dma_start(run[:], prev[rows, :].rearrange("(t p) j -> p t j", p=P))
+            prev_sb.extend(run[:, i, :] for i in range(count))
 
         w1_codes = {}
         w1_planes = {}
@@ -255,7 +256,7 @@ def tile_list_tabmlp_res_kernel(tc, tab, w1, w2_words, w2_scales, prev, offs, ou
                         start=(b == 0),
                         stop=(b == HB - 1),
                     )
-                before = prev_sb[n // PREV_TILES][:, n % PREV_TILES, cols]
+                before = prev_sb[n][:, cols]
                 nc.vector.tensor_tensor(result[:, i, :], bank[:], before, ADD)
                 if turn == 0:
                     quantize_h(1, 1, h_last[:, SIDE:S], 3, 1)

@@ -237,33 +237,27 @@ def tile_list_tabmlp_res_kernel(tc, tab, w1, w2_words, w2_scales, prev, offs, ou
             if g == 6:
                 quantize_h(1, 1, h_last[:, SIDE:S], 2, 1)
 
-        dead_slots = [f"w1_raw_0_{a}" for a in range(KA)] + [f"tab_words_{a}" for a in range(KA)] + ["w1_raw_1_0", "w1_raw_1_1"]
-        stores = [[(n, s) for n in range(2)] for s in range(SIDES)]
-        stores.extend([(n, s) for s in range(SIDES)] for n in range(2, NT))
-        turn = 0
-        for u, sums in enumerate(stores):
-            result = keep.tile([P, 2, SIDE], F32, name=dead_slots[u], align_bytes=256)
-            for i, (n, s) in enumerate(sums):
-                cols = slice(SIDE * s, SIDE * (s + 1))
-                bank = psum.tile([P, SIDE], F32, name=f"bank{turn % BANKS}")
-                for b in range(HB):
-                    nc.tensor.matmul_mx(
-                        out=bank[:],
-                        lhsT=w2_codes[:, b, :].bitcast(U8)[:, 256 * n : 256 * (n + 1)].bitcast(FP4X4),
-                        lhsT_scale=w2_planes[:, b, :].bitcast(U8)[:, P * n : P * (n + 1)],
-                        rhs=h_codes[b, s].bitcast(FP8X4),
-                        rhs_scale=h_planes[b, s],
-                        start=(b == 0),
-                        stop=(b == HB - 1),
-                    )
-                before = prev_sb[n][:, cols]
-                nc.vector.tensor_tensor(result[:, i, :], bank[:], before, ADD)
-                if turn == 0:
-                    quantize_h(1, 1, h_last[:, SIDE:S], 3, 1)
-                turn += 1
-            if u < SIDES:
-                target = out[0 : 2 * P, SIDE * u : SIDE * (u + 1)].rearrange("(t p) j -> p t j", p=P)
-            else:
-                target = out[P * u : P * (u + 1), :].rearrange("p (s j) -> p s j", s=SIDES)
-            queue = nc.scalar if u == NT - 1 else nc.sync
-            queue.dma_start(target, result[:])
+        dead_slots = [f"w1_raw_{b}_{a}" for b in range(HB) for a in range(KA)] + [f"tab_words_{a}" for a in range(KA)]
+        sums = [(n, s) for s in range(SIDES) for n in range(2)]
+        sums.extend((n, s) for n in range(2, NT) for s in range(SIDES))
+        for turn, (n, s) in enumerate(sums):
+            if turn % 2 == 0:
+                pair = keep.tile([P, 2, SIDE], F32, name=dead_slots[turn // 2], align_bytes=256)
+            result = pair[:, turn % 2, :]
+            cols = slice(SIDE * s, SIDE * (s + 1))
+            bank = psum.tile([P, SIDE], F32, name=f"bank{turn % BANKS}")
+            for b in range(HB):
+                nc.tensor.matmul_mx(
+                    out=bank[:],
+                    lhsT=w2_codes[:, b, :].bitcast(U8)[:, 256 * n : 256 * (n + 1)].bitcast(FP4X4),
+                    lhsT_scale=w2_planes[:, b, :].bitcast(U8)[:, P * n : P * (n + 1)],
+                    rhs=h_codes[b, s].bitcast(FP8X4),
+                    rhs_scale=h_planes[b, s],
+                    start=(b == 0),
+                    stop=(b == HB - 1),
+                )
+            nc.vector.tensor_tensor(result, bank[:], prev_sb[n][:, cols], ADD)
+            if turn == 0:
+                quantize_h(1, 1, h_last[:, SIDE:S], 3, 1)
+            queue = nc.scalar if turn == len(sums) - 1 else nc.sync
+            queue.dma_start(out[P * n : P * (n + 1), cols], result)

from contextlib import ExitStack

import concourse.mybir as mybir

K, H, M, T, S = 1536, 1024, 1024, 2048, 1024
FLOPS = 2 * K * H * S + 2 * H * M * S

F32 = mybir.dt.float32
BF16 = mybir.dt.bfloat16
I32 = mybir.dt.int32
U32 = mybir.dt.uint32
U16 = mybir.dt.uint16
U8 = mybir.dt.uint8
FP8X4 = mybir.dt.float8_e4m3fn_x4
FP4X4 = mybir.dt.float4_e2m1fn_x4
RELU = mybir.ActivationFunctionType.Relu
ADD = mybir.AluOpType.add

P = 128
PASS = 512
KA = K // PASS
HB = H // PASS
SIDE = 512
SIDES = S // SIDE
NT = M // P
BANKS = 8
PREV_RUNS = (2, 3, 3)


def tile_list_tabmlp_res_kernel(tc, tab, w1, w2_words, w2_scales, prev, offs, out):
    nc = tc.nc
    with ExitStack() as ctx:
        keep = ctx.enter_context(tc.tile_pool(name="keep", bufs=1))
        psum = ctx.enter_context(tc.psum_pool(name="psum", bufs=1))

        def staggered(columns, dtype, size, shift, name):
            padded = keep.tile([P, columns + shift // size], dtype, name=name, align_bytes=256)
            return padded[:, shift // size :]

        offsets = keep.tile([P, S // 16], U16, name="offsets")
        tab_scales = keep.tile([P, T // 4], I32, name="tab_scales", align_bytes=256)
        nc.vector.memset(tab_scales[:], 0)
        w2_planes = staggered(HB * M // 4, I32, 4, 192, "w2_planes")
        nc.vector.memset(w2_planes, 0)
        w2_planes = w2_planes.rearrange("p (b x) -> p b x", b=HB)
        tab_bytes = tab[:, PASS * T :].rearrange("a (q t) -> a q t", t=T)

        tab_words = {}
        w1_raw = {}

        def load_tab(a):
            tab_words[a] = keep.tile([P, T], I32, name=f"tab_words_{a}", align_bytes=256)
            nc.sync.dma_start(tab_words[a][:], tab[a, 0 : PASS * T].rearrange("(p x) -> p x", p=P).bitcast(I32))

        def load_w1(b, a):
            w1_raw[b, a] = keep.tile([P, 4, PASS], F32, name=f"w1_raw_{b}_{a}", align_bytes=256)
            nc.sync.dma_start(
                w1_raw[b, a][:],
                w1[PASS * a : PASS * (a + 1), PASS * b : PASS * (b + 1)].rearrange("(p j) c -> p j c", j=4),
            )

        load_tab(0)
        nc.sync.dma_start(offsets[:], offs)
        load_w1(0, 0)
        for q in range(4):
            nc.sync.dma_start(
                tab_scales[32 * q + 4 : 32 * q + 4 + 4 * KA, :],
                tab_bytes[:, 4 * q : 4 * q + 4, :].bitcast(I32),
            )
        for a in range(1, KA):
            load_w1(0, a)
            load_tab(a)
        for a in range(KA):
            load_w1(1, a)
        w2_codes = staggered(HB * M // 2, I32, 4, 128, "w2_codes").rearrange("p (b x) -> p b x", b=HB)
        nc.sync.dma_start(w2_codes, w2_words.rearrange("b p x -> p b x").bitcast(I32))
        for r in range(4):
            nc.sync.dma_start(
                w2_planes[r:P:32, :, :],
                w2_scales[:, r:16:4, :].rearrange("b q n -> q b n").bitcast(I32),
            )
        prev_sb = []
        for u, count in enumerate(PREV_RUNS):
            run = keep.tile([P, count, S], F32, name=f"prev_{u}", align_bytes=256)
            rows = slice(P * len(prev_sb), P * (len(prev_sb) + count))
            nc.sync.dma_start(run[:], prev[rows, :].rearrange("(t p) j -> p t j", p=P))
            prev_sb.extend(run[:, i, :] for i in range(count))

        w1_codes = {}
        w1_planes = {}
        w1_grouped = {}

        def lay_out(b, a, u, on_scalar):
            grouped = keep.tile([P, 2, P, 4], BF16, name=f"grouped_{b}_{a}_{u}", align_bytes=256)
            w1_grouped[b, a, u] = grouped[:]
            src = w1_raw[b, a][:].rearrange("p j (m t) -> p m j t", t=4)[:, :, :, 2 * u : 2 * u + 2]
            dst = grouped[:].rearrange("p t m j -> p m j t")
            if on_scalar > 0:
                nc.scalar.copy(dst[:, 0:on_scalar], src[:, 0:on_scalar])
            if on_scalar < P:
                nc.vector.tensor_copy(dst[:, on_scalar:P], src[:, on_scalar:P])

        def quantize_w1(b, a, u):
            slot = "w1_raw_0_2" if (b, a, u) == (0, 1, 1) else f"w1_codes_{b}_{a}_{u}"
            w1_codes[b, a, u] = staggered(2 * P, U32, 4, 128, slot)
            w1_planes[b, a, u] = staggered(2 * P, U8, 1, 192, f"w1_planes_{b}_{a}_{u}")
            nc.vector.quantize_mx(
                out=w1_codes[b, a, u].bitcast(FP8X4),
                scales=w1_planes[b, a, u],
                in_=w1_grouped[b, a, u].rearrange("p t m j -> p (t m j)"),
            )

        def prepare_w1(b, a, on_scalar):
            lay_out(b, a, 0, 0)
            lay_out(b, a, 1, on_scalar)
            quantize_w1(b, a, 0)
            quantize_w1(b, a, 1)

        picked = {}
        picked_scales = {}

        def gather_words(a, s, n):
            picked[a, s] = keep.tile([P, SIDE], U32, name=f"picked_{a}_{s}", align_bytes=256)
            for c0 in range(0, SIDE, n):
                first = (SIDE * s + c0) // 16
                nc.vector.tensor_copy(
                    picked[a, s][:, c0 : c0 + n],
                    tab_words[a][:].bitcast(U32).indirect(offsets[:, first : first + n // 16]),
                )

        def gather_scales(s):
            picked_scales[s] = staggered(SIDE, U8, 1, 64, f"picked_scales_{s}")
            nc.vector.tensor_copy(
                picked_scales[s],
                tab_scales[:].bitcast(U8).indirect(offsets[:, 32 * s : 32 * (s + 1)]),
            )

        passes_done = {}

        def layer1(banks, b, a, order):
            for g, j in order:
                cols = slice(P * (g % 4), P * (g % 4 + 1))
                part = slice(P * (j % 2), P * (j % 2 + 1))
                done = passes_done.get((b, g), 0)
                passes_done[b, g] = done + 1
                nc.tensor.matmul_mx(
                    out=banks[g][:, j, :],
                    lhsT=w1_codes[b, a, j // 2][:, part].bitcast(FP8X4),
                    lhsT_scale=w1_planes[b, a, j // 2][:, part],
                    rhs=picked[a, g // 4][:, cols].bitcast(FP8X4),
                    rhs_scale=picked_scales[g // 4][4 * (a + 1) : P, cols],
                    start=(done == 0),
                    stop=(done == 4 * KA - 1),
                )

        def across(gs, js):
            return [(g, j) for j in js for g in gs]

        def within(g, js):
            return [(g, j) for j in (js if g % 2 == 0 else reversed(js))]

        h_grouped = {}
        h_codes = {}
        h_planes = {}

        def rectify(bank, b, g, on_vector):
            if g % 4 == 0:
                h_grouped[b, g // 4] = keep.tile([P, SIDE, 4], BF16, name=f"h_grouped_{b}_{g // 4}", align_bytes=256)
            dst = h_grouped[b, g // 4][:, P * (g % 4) : P * (g % 4 + 1), :]
            src = bank[:].rearrange("p j n -> p n j")
            if on_vector:
                nc.vector.tensor_scalar_max(dst, src, 0.0)
            else:
                nc.scalar.activation(dst, src, RELU)

        def quantize_h(b, s, codes, first=0, count=4):
            if first == 0:
                h_codes[b, s] = codes
                h_planes[b, s] = staggered(SIDE, U8, 1, 64, f"h_planes_{b}_{s}")
            cols = slice(P * first, P * (first + count))
            nc.vector.quantize_mx(
                out=codes[:, cols].bitcast(FP8X4),
                scales=h_planes[b, s][:, cols],
                in_=h_grouped[b, s][:, cols, :].rearrange("p n j -> p (n j)"),
            )

        banks = [psum.tile([P, 4, P], F32, name=f"bank{g}") for g in range(BANKS)]
        for s in range(SIDES):
            gather_words(0, s, SIDE)
        prepare_w1(0, 0, P)
        for s in range(SIDES):
            gather_scales(s)
            layer1(banks, 0, 0, across(range(4 * s, 4 * s + 4), range(4)))
        lay_out(0, 1, 0, P)
        lay_out(0, 1, 1, P)
        quantize_w1(0, 1, 0)
        for s in range(SIDES):
            gather_words(1, s, SIDE)
            layer1(banks, 0, 1, across(range(4 * s, 4 * s + 4), range(2)))
        lay_out(0, 2, 0, 0)
        lay_out(0, 2, 1, P)
        quantize_w1(0, 2, 0)
        quantize_w1(0, 1, 1)
        quantize_w1(0, 2, 1)
        layer1(banks, 0, 1, across(range(BANKS), range(2, 4)))
        for s in range(SIDES):
            gather_words(2, s, SIDE // 2)
            for g in range(4 * s, 4 * s + 4):
                layer1(banks, 0, 2, within(g, range(4)))
                rectify(banks[g], 0, g, False)

        banks = [psum.tile([P, 4, P], F32, name=f"bank{g}") for g in range(BANKS)]
        prepare_w1(1, 0, 0)
        layer1(banks, 1, 0, across(range(3), range(2)))
        layer1(banks, 1, 0, across(range(3), range(2, 4)))
        for g in range(3, BANKS):
            layer1(banks, 1, 0, within(g, range(4)))
        prepare_w1(1, 1, 0)
        layer1(banks, 1, 1, across(range(4), range(4)))
        prepare_w1(1, 2, P)
        held = keep.tile([P, SIDE], U32, name="grouped_1_2_1", align_bytes=256)
        quantize_h(0, 0, held[:])
        h_last = keep.tile([P, S], U32, name="h_last", align_bytes=256)
        layer1(banks, 1, 2, across(range(4), range(2)))
        for g in range(4):
            layer1(banks, 1, 2, within(g, range(2, 4)))
            rectify(banks[g], 1, g, g % 2 == 1)
        quantize_h(1, 0, h_last[:, 0:SIDE])
        held = keep.tile([P, SIDE], U32, name="h_grouped_1_0", align_bytes=256)
        quantize_h(0, 1, held[:])
        for g in range(4, BANKS):
            for a in (2, 1):
                layer1(banks, 1, a, within(g, range(4)))
            rectify(banks[g], 1, g, False)
            if g == 5:
                quantize_h(1, 1, h_last[:, SIDE:S], 0, 2)
            if g == 6:
                quantize_h(1, 1, h_last[:, SIDE:S], 2, 1)

        dead_slots = [f"w1_raw_{b}_{a}" for b in range(HB) for a in range(KA)] + [f"tab_words_{a}" for a in range(KA)]
        sums = [(n, s) for s in range(SIDES) for n in range(2)]
        sums.extend((n, s) for n in range(2, NT) for s in range(SIDES))
        for turn, (n, s) in enumerate(sums):
            if turn % 2 == 0:
                pair = keep.tile([P, 2, SIDE], F32, name=dead_slots[turn // 2], align_bytes=256)
            result = pair[:, turn % 2, :]
            cols = slice(SIDE * s, SIDE * (s + 1))
            bank = psum.tile([P, SIDE], F32, name=f"bank{turn % BANKS}")
            for b in range(HB):
                nc.tensor.matmul_mx(
                    out=bank[:],
                    lhsT=w2_codes[:, b, :].bitcast(U8)[:, 256 * n : 256 * (n + 1)].bitcast(FP4X4),
                    lhsT_scale=w2_planes[:, b, :].bitcast(U8)[:, P * n : P * (n + 1)],
                    rhs=h_codes[b, s].bitcast(FP8X4),
                    rhs_scale=h_planes[b, s],
                    start=(b == 0),
                    stop=(b == HB - 1),
                )
            nc.vector.tensor_tensor(result, bank[:], prev_sb[n][:, cols], ADD)
            if turn == 0:
                quantize_h(1, 1, h_last[:, SIDE:S], 3, 1)
            queue = nc.scalar if turn == len(sums) - 1 else nc.sync
            queue.dma_start(out[P * n : P * (n + 1), cols], result)
